import numpy as np
import ml_dtypes


def mxq(x, axis, fmt="e4m3"):
    dtype, down = {"e4m3": (ml_dtypes.float8_e4m3fn, 7), "e5m2": (ml_dtypes.float8_e5m2, 14)}[fmt]
    v = np.moveaxis(np.asarray(x, np.float32).astype(ml_dtypes.bfloat16).astype(np.float64), axis, -1)
    blocks = v.reshape(v.shape[:-1] + (-1, 32))
    amax = np.abs(blocks).max(-1, keepdims=True)
    byte = np.maximum(np.where(amax > 0, np.frexp(amax)[1] - 1 + 127, 0) - down, 1)
    scale = np.exp2(byte - 127.0)
    codes = (blocks / scale).astype(np.float32).astype(dtype).astype(np.float64)
    return np.moveaxis((codes * scale).reshape(v.shape), -1, axis)


WIDE = False


def mx_kscale(k):
    if not WIDE:
        return np.ones(k)
    levels = np.array([10, -10, 5, -5, 0])
    if k % 512:
        return np.exp2(np.random.permutation(np.resize(levels, k // 32))).repeat(32)
    a = np.empty((k // 512, 16))
    for p in range(k // 512):
        a[p, :8] = np.random.permutation(np.resize(levels, 8))
        for g in range(8):
            far = levels[np.abs(levels - a[p, g]) >= 10]
            a[p, g + 8] = far[np.random.randint(len(far))]
    return np.exp2(a.ravel()).repeat(32)


def f64(x):
    return np.asarray(x).astype(np.float64)


def striped(idx):
    return np.tile(idx.reshape(-1, 16).T, (8, 1)).astype(np.uint16)


def unstriped(offs):
    return offs[:16].T.reshape(-1).astype(np.int64)


def pack_weight(w):
    k, n = w.shape
    w = f64(np.asarray(w, np.float32).astype(ml_dtypes.bfloat16)).reshape(k // 32, 32, n)
    amax = np.abs(w).max(1)
    byte = np.clip(np.where(amax > 0, np.frexp(amax)[1] - 1 + 127 - 7, 1), 1, 254)
    scaled = (w * np.exp2(127.0 - byte)[:, None, :]).reshape(k, n).astype(np.float32)
    words = np.ascontiguousarray(scaled.reshape(k // 512, 128, 4, n).transpose(0, 1, 3, 2)).astype(ml_dtypes.float8_e4m3fn).view(np.uint8)
    return words, np.ascontiguousarray(byte.astype(np.uint8).reshape(k // 512, 16, n))


def unpack_weight(words, scales):
    g, p, n, _ = words.shape
    vals = np.ascontiguousarray(words).view(ml_dtypes.float8_e4m3fn).astype(np.float64) * np.repeat(np.exp2(scales.astype(np.float64) - 127.0), 8, axis=1)[..., None]
    return vals.transpose(0, 1, 3, 2).reshape(g * 512, n)


def planes(y):
    n, m = y.shape
    v = y.astype(np.float32).astype(ml_dtypes.bfloat16).astype(np.float64).reshape(n // 32, 32, m)
    top = np.abs(v).max(1)
    byte = np.clip(np.where(top > 0, np.frexp(top)[1] - 1 + 127 - 7, 1), 1, 254)
    codes = (v * np.exp2(127.0 - byte)[:, None, :]).reshape(n, m).astype(np.float32).astype(ml_dtypes.float8_e4m3fn).view(np.uint8)
    words = codes.reshape(n // 512, 128, 4, m).transpose(0, 1, 3, 2)
    return np.ascontiguousarray(words), np.ascontiguousarray(byte.astype(np.uint8).reshape(n // 512, 16, m))


def relu(v):
    return np.maximum(v, 0.0)


K, T, S, D, V, H = 512, 1024, 512, 2, 256, 512
P = 2 ** 7


def setup_inputs():
    n = np.random.standard_normal
    s = mx_kscale(K)[:, None]
    u = mx_kscale(H)
    near = np.random.permutation(S)
    packed_xT = pack_weight(n((K, T)) * s)
    return {
        "x_words": packed_xT[0],
        "x_scales": packed_xT[1],
        "w1": (n((K, H)) / np.sqrt(K) / s * u).astype(np.float32),
        "w2": (n((H, H)) / np.sqrt(H) / u[:, None]).astype(np.float32),
        "gate": (np.tile(np.random.uniform(0.2, 1.0, (D, 1, V)) / np.sqrt(D), (1, P, 1))).astype(np.float32),
        "turn": (np.random.uniform(0.5, 1.5, (H, 1)) * u[:, None]).astype(np.float32),
        "offs": striped(np.random.permutation(T)[:S]),
        "cen": striped(np.random.permutation(S)[:V]),
        "pos1": striped(near[:V]),
        "pos2": striped(near[V:]),
    }


def reference(x_words, x_scales, w1, w2, gate, turn, offs, cen, pos1, pos2):
    xq = unpack_weight(x_words, x_scales)[:, unstriped(offs)]
    h = relu(mxq(f64(w1), 0, "e4m3").T @ xq)
    z = 0.9 * (h[:, unstriped(pos1)] * f64(gate)[0, :1] + h[:, unstriped(pos2)] * f64(gate)[1, :1]) + 0.1 * h[:, unstriped(cen)]
    y = mxq(f64(w2), 0, "e4m3").T @ mxq(z, 0, "e4m3")
    out_0 = 0.6 * z + 0.4 * (f64(turn) * y)
    return (out_0,) + planes(out_0)

@@ -1,0 +1,172 @@
+from contextlib import ExitStack
+
+import concourse.mybir as mybir
+
+K, T, S, V, H = 512, 1024, 512, 256, 512
+FLOPS = 2 * K * H * S + 2 * H * H * V
+
+F32 = mybir.dt.float32
+BF16 = mybir.dt.bfloat16
+I32 = mybir.dt.int32
+U32 = mybir.dt.uint32
+U16 = mybir.dt.uint16
+U8 = mybir.dt.uint8
+FP8X4 = mybir.dt.float8_e4m3fn_x4
+ALU = mybir.AluOpType
+ACT = mybir.ActivationFunctionType
+
+P = 128
+PACK = 4
+BLOCKS = [(0, 128), (128, 128)]
+
+
+def deal(engine_copy, grouped, raw, m0, m1, m_base):
+    engine_copy(
+        out=grouped[:, :, m0:m1, :].rearrange("p t m j -> p m j t"),
+        in_=raw[:].rearrange("p j (m t) -> p m j t", t=PACK)[:, m0 - m_base : m1 - m_base, :, :],
+    )
+
+
+def tile_picked_zgcnii_relu_po_kernel(
+    tc, x_words, x_scales, w1, w2, gate, turn, offs, cen, pos1, pos2, out_0, out_1, out_2
+):
+    nc = tc.nc
+    with ExitStack() as ctx:
+        keep = ctx.enter_context(tc.tile_pool(name="keep", bufs=1))
+        psum = ctx.enter_context(tc.psum_pool(name="psum", bufs=1))
+
+        offs_sb = keep.tile([P, S // 16], U16, name="offs_sb")
+        cen_sb = keep.tile([P, V // 16], U16, name="cen_sb")
+        pos1_sb = keep.tile([P, V // 16], U16, name="pos1_sb")
+        pos2_sb = keep.tile([P, V // 16], U16, name="pos2_sb")
+        xw = keep.tile([P, T], U32, name="xw")
+        xs = keep.tile([P, T], U8, name="xs")
+        half = H // 2
+        w1_raw = [keep.tile([P, PACK, half], F32, name="w1_raw%d" % a) for a in range(2)]
+        w2_raw = keep.tile([P, PACK, H], F32, name="w2_raw")
+        gate_sb = keep.tile([P, 2, V], F32, name="gate_sb")
+        turn_sb = keep.tile([P, PACK], F32, name="turn_sb")
+
+        nc.vector.memset(xs[:].bitcast(I32), 0)
+        nc.sync.dma_start(offs_sb[:], offs)
+        nc.sync.dma_start(pos1_sb[:], pos1)
+        nc.sync.dma_start(pos2_sb[:], pos2)
+        nc.sync.dma_start(xw[:].bitcast(I32), x_words[0].rearrange("p c r -> p (c r)").bitcast(I32))
+        for q in range(4):
+            nc.scalar.dma_start(xs[32 * q : 32 * q + 4, :].bitcast(I32), x_scales[0][4 * q : 4 * q + 4, :].bitcast(I32))
+        w1_rows = w1.rearrange("(p j) c -> p j c", j=PACK)
+        for a in range(2):
+            nc.sync.dma_start(w1_raw[a][:], w1_rows[:, :, a * half : (a + 1) * half])
+        nc.sync.dma_start(cen_sb[:], cen)
+        nc.sync.dma_start(gate_sb[:], gate.rearrange("d p v -> p d v"))
+        nc.sync.dma_start(w2_raw[:], w2.rearrange("(p j) c -> p j c", j=PACK))
+        nc.sync.dma_start(turn_sb[:], turn.rearrange("(p t) o -> p (t o)", t=PACK))
+
+        xg_w = keep.tile([P, S], U32, name="xg_w", align_bytes=64)
+        xg_s = keep.tile([P, S], U8, name="xg_s", align_bytes=64)
+        nc.vector.tensor_copy(xg_w[:], xw[:].indirect(offs_sb[:]))
+        nc.vector.tensor_copy(xg_s[:], xs[:].indirect(offs_sb[:]))
+
+        w1_bf = keep.tile([P, PACK, P, PACK], BF16, name="w1_bf", align_bytes=64)
+        w1_w = keep.tile([P, H], U32, name="w1_w", align_bytes=64)
+        w1_s = keep.tile([P, H], U8, name="w1_s", align_bytes=64)
+        deal(nc.scalar.copy, w1_bf, w1_raw[0], 0, 64, 0)
+        deal(nc.scalar.copy, w1_bf, w1_raw[1], 64, 84, 64)
+        deal(nc.vector.tensor_copy, w1_bf, w1_raw[1], 84, 128, 64)
+
+        h = []
+        for t in range(PACK):
+            cols = slice(t * P, (t + 1) * P)
+            nc.vector.quantize_mx(
+                out=w1_w[:, cols].bitcast(FP8X4),
+                scales=w1_s[:, cols],
+                in_=w1_bf[:, t, :, :].rearrange("p m j -> p (m j)"),
+            )
+            acc = psum.tile([P, S], F32, name="h_acc%d" % t)
+            nc.tensor.matmul_mx(
+                out=acc[:], lhsT=w1_w[:, cols].bitcast(FP8X4), lhsT_scale=w1_s[:, cols],
+                rhs=xg_w[:].bitcast(FP8X4), rhs_scale=xg_s[:], start=True, stop=True,
+            )
+            h_t = keep.tile([P, S], F32, name="h%d" % t)
+            nc.scalar.activation(h_t[:], acc[:], ACT.Relu, scale=0.06)
+            h.append(h_t)
+
+        w2_bf = keep.tile([P, PACK, P, PACK], BF16, name="w2_bf", align_bytes=64)
+        w2_w = keep.tile([P, H], U32, name="w2_w", align_bytes=64)
+        w2_s = keep.tile([P, H], U8, name="w2_s", align_bytes=64)
+        turn4 = keep.tile([P, PACK], F32, name="turn4")
+        y_w = keep.tile([P, V], U32, name="y_w", align_bytes=64)
+        y_s = keep.tile([P, V], U8, name="y_s", align_bytes=64)
+        out_rows = out_0.rearrange("(p t) v -> p t v", t=PACK)
+        out_words = out_1[0].rearrange("p c r -> p (c r)").bitcast(I32)
+
+        def gathers(b):
+            v0, w = BLOCKS[b]
+            lst = slice(v0 // 16, (v0 + w) // 16)
+            ga = keep.tile([P, PACK, w], F32, name="ga%d" % b)
+            gb = keep.tile([P, PACK, w], F32, name="gb%d" % b)
+            gc = keep.tile([P, PACK, w], F32, name="gc%d" % b)
+            u = keep.tile([P, PACK, w], F32, name="u%d" % b)
+
+            def mix(ts):
+                nc.vector.tensor_tensor(ga[:, ts, :], ga[:, ts, :], gb[:, ts, :], ALU.add)
+
+            def finish(ts):
+                nc.vector.scalar_tensor_tensor(u[:, ts, :], ga[:, ts, :], 9.0, gc[:, ts, :], ALU.mult, ALU.add)
+
+            for t in range(PACK):
+                nc.vector.tensor_tensor(ga[:, t, :], h[t][:].indirect(pos1_sb[:, lst]), gate_sb[:, 0, v0 : v0 + w], ALU.mult)
+                nc.vector.tensor_tensor(gb[:, t, :], h[t][:].indirect(pos2_sb[:, lst]), gate_sb[:, 1, v0 : v0 + w], ALU.mult)
+                if t == PACK - 1:
+                    mix(slice(0, PACK - 1))
+                nc.vector.tensor_copy(gc[:, t, :], h[t][:].indirect(cen_sb[:, lst]))
+            mix(slice(PACK - 1, PACK))
+            finish(slice(0, PACK - 1))
+            finish(slice(PACK - 1, PACK))
+            return u
+
+        def interleave(dst, src, scale):
+            nc.scalar.activation(
+                dst[:].rearrange("p (c i) t -> p c t i", i=4),
+                src[:].rearrange("p t (c i) -> p c t i", i=4),
+                ACT.Copy, scale=scale,
+            )
+
+        def second(b, u):
+            v0, w = BLOCKS[b]
+            z_bf = keep.tile([P, w, PACK], BF16, name="z_bf%d" % b, align_bytes=64)
+            z_w = keep.tile([P, w], U32, name="z_w%d" % b, align_bytes=64)
+            z_s = keep.tile([P, w], U8, name="z_s%d" % b, align_bytes=64)
+            interleave(z_bf, u, 1.0 / 0.6)
+            nc.vector.quantize_mx(out=z_w[:].bitcast(FP8X4), scales=z_s[:], in_=z_bf[:].rearrange("p v t -> p (v t)"))
+            y = psum.tile([P, PACK, w], F32, name="y%d" % b)
+            res = keep.tile([P, PACK, w], F32, name="res%d" % b)
+            for t in range(PACK):
+                cols = slice(t * P, (t + 1) * P)
+                nc.tensor.matmul_mx(
+                    out=y[:, t, :], lhsT=w2_w[:, cols].bitcast(FP8X4), lhsT_scale=w2_s[:, cols],
+                    rhs=z_w[:].bitcast(FP8X4), rhs_scale=z_s[:], start=True, stop=True,
+                )
+            for t in range(PACK):
+                nc.vector.scalar_tensor_tensor(res[:, t, :], y[:, t, :], turn4[:, t : t + 1], u[:, t, :], ALU.mult, ALU.add)
+            nc.sync.dma_start(out_rows[:, :, v0 : v0 + w], res[:])
+            res_bf = keep.tile([P, w, PACK], BF16, name="res_bf%d" % b, align_bytes=64)
+            interleave(res_bf, res, 1.0)
+            nc.vector.quantize_mx(
+                out=y_w[:, v0 : v0 + w].bitcast(FP8X4), scales=y_s[:, v0 : v0 + w],
+                in_=res_bf[:].rearrange("p v t -> p (v t)"),
+            )
+            nc.sync.dma_start(out_words[:, v0 : v0 + w], y_w[:, v0 : v0 + w].bitcast(I32))
+
+        u0 = gathers(0)
+        deal(nc.scalar.copy, w2_bf, w2_raw, 0, P, 0)
+        nc.scalar.activation(turn4[:], turn_sb[:], ACT.Copy, scale=0.4)
+        nc.vector.quantize_mx(
+            out=w2_w[:].bitcast(FP8X4), scales=w2_s[:], in_=w2_bf[:].rearrange("p t m j -> p (t m j)")
+        )
+        second(0, u0)
+        u1 = gathers(1)
+        second(1, u1)
+        for q in range(4):
+            queue = nc.sync if q % 2 == 0 else nc.scalar
+            queue.dma_start(out_2[0][4 * q : 4 * q + 4, :].bitcast(I32), y_s[32 * q : 32 * q + 4, :].bitcast(I32))

@@ -1,6 +1,7 @@
 from contextlib import ExitStack
 
 import concourse.mybir as mybir
+from concourse.masks import make_identity
 
 K, T, S, V, H = 512, 1024, 512, 256, 512
 FLOPS = 2 * K * H * S + 2 * H * H * V
@@ -17,7 +18,9 @@ ACT = mybir.ActivationFunctionType
 
 P = 128
 PACK = 4
-BLOCKS = [(0, 128), (128, 128)]
+BW = 128
+NB = V // BW
+EARLY = 3
 
 
 def deal(engine_copy, grouped, raw, m0, m1, m_base):
@@ -41,105 +44,124 @@ def tile_picked_zgcnii_relu_po_kernel(
         pos2_sb = keep.tile([P, V // 16], U16, name="pos2_sb")
         xw = keep.tile([P, T], U32, name="xw")
         xs = keep.tile([P, T], U8, name="xs")
-        half = H // 2
-        w1_raw = [keep.tile([P, PACK, half], F32, name="w1_raw%d" % a) for a in range(2)]
+        w1_raw = keep.tile([P, PACK, H], F32, name="w1_raw")
         w2_raw = keep.tile([P, PACK, H], F32, name="w2_raw")
-        gate_sb = keep.tile([P, 2, V], F32, name="gate_sb")
-        turn_sb = keep.tile([P, PACK], F32, name="turn_sb")
+        turn_raw = keep.tile([P, PACK], F32, name="turn_raw")
+        xs_rows = keep.tile([P, T], U8, name="xs_rows")
+        gate_raw = keep.tile([P, 2, V], F32, name="gate_raw")
+        ident = keep.tile([P, P], F32, name="ident")
 
-        nc.vector.memset(xs[:].bitcast(I32), 0)
+        quadrants = [slice(32 * q, 32 * q + 4) for q in range(4)]
+        for q in range(4):
+            queue = nc.scalar if q < 2 else nc.sync
+            queue.dma_start(xs_rows[quadrants[q], :].bitcast(I32), x_scales[0][4 * q : 4 * q + 4, :].bitcast(I32))
         nc.sync.dma_start(offs_sb[:], offs)
+        nc.sync.dma_start(w1_raw[:], w1.rearrange("(p j) c -> p j c", j=PACK))
+        nc.sync.dma_start(xw[:].bitcast(I32), x_words[0].rearrange("p c r -> p (c r)").bitcast(I32))
+        nc.sync.dma_start(cen_sb[:], cen)
         nc.sync.dma_start(pos1_sb[:], pos1)
         nc.sync.dma_start(pos2_sb[:], pos2)
-        nc.sync.dma_start(xw[:].bitcast(I32), x_words[0].rearrange("p c r -> p (c r)").bitcast(I32))
-        for q in range(4):
-            nc.scalar.dma_start(xs[32 * q : 32 * q + 4, :].bitcast(I32), x_scales[0][4 * q : 4 * q + 4, :].bitcast(I32))
-        w1_rows = w1.rearrange("(p j) c -> p j c", j=PACK)
-        for a in range(2):
-            nc.sync.dma_start(w1_raw[a][:], w1_rows[:, :, a * half : (a + 1) * half])
-        nc.sync.dma_start(cen_sb[:], cen)
-        nc.sync.dma_start(gate_sb[:], gate.rearrange("d p v -> p d v"))
+        nc.sync.dma_start(gate_raw[:], gate.rearrange("d p v -> p d v"))
+        nc.sync.dma_start(turn_raw[:], turn.rearrange("(p t) o -> p (t o)", t=PACK))
         nc.sync.dma_start(w2_raw[:], w2.rearrange("(p j) c -> p j c", j=PACK))
-        nc.sync.dma_start(turn_sb[:], turn.rearrange("(p t) o -> p (t o)", t=PACK))
+        make_identity(nc, ident[:])
 
+        nc.vector.memset(xs[:].bitcast(I32), 0)
+        for q in range(4):
+            nc.vector.tensor_copy(xs[quadrants[q], :].bitcast(I32), xs_rows[quadrants[q], :].bitcast(I32))
         xg_w = keep.tile([P, S], U32, name="xg_w", align_bytes=64)
         xg_s = keep.tile([P, S], U8, name="xg_s", align_bytes=64)
-        nc.vector.tensor_copy(xg_w[:], xw[:].indirect(offs_sb[:]))
         nc.vector.tensor_copy(xg_s[:], xs[:].indirect(offs_sb[:]))
 
         w1_bf = keep.tile([P, PACK, P, PACK], BF16, name="w1_bf", align_bytes=64)
         w1_w = keep.tile([P, H], U32, name="w1_w", align_bytes=64)
         w1_s = keep.tile([P, H], U8, name="w1_s", align_bytes=64)
-        deal(nc.scalar.copy, w1_bf, w1_raw[0], 0, 64, 0)
-        deal(nc.scalar.copy, w1_bf, w1_raw[1], 64, 84, 64)
-        deal(nc.vector.tensor_copy, w1_bf, w1_raw[1], 84, 128, 64)
+        deal(nc.scalar.copy, w1_bf, w1_raw, 0, 44, 0)
+        deal(nc.vector.tensor_copy, w1_bf, w1_raw, 44, P, 0)
+        gate9 = keep.tile([P, 2, V], F32, name="gate9")
 
-        h = []
-        for t in range(PACK):
+        def quantize_w1(t):
             cols = slice(t * P, (t + 1) * P)
             nc.vector.quantize_mx(
                 out=w1_w[:, cols].bitcast(FP8X4),
                 scales=w1_s[:, cols],
                 in_=w1_bf[:, t, :, :].rearrange("p m j -> p (m j)"),
             )
-            acc = psum.tile([P, S], F32, name="h_acc%d" % t)
+
+        def first_product(t, entries, tag):
+            cols = slice(t * P, (t + 1) * P)
+            acc = psum.tile([P, entries.stop - entries.start], F32, name="h_acc", tag=tag)
             nc.tensor.matmul_mx(
                 out=acc[:], lhsT=w1_w[:, cols].bitcast(FP8X4), lhsT_scale=w1_s[:, cols],
-                rhs=xg_w[:].bitcast(FP8X4), rhs_scale=xg_s[:], start=True, stop=True,
+                rhs=xg_w[:, entries].bitcast(FP8X4), rhs_scale=xg_s[:, entries], start=True, stop=True,
             )
-            h_t = keep.tile([P, S], F32, name="h%d" % t)
-            nc.scalar.activation(h_t[:], acc[:], ACT.Relu, scale=0.06)
-            h.append(h_t)
+            return acc
+
+        h = [keep.tile([P, S], F32, name="h%d" % t) for t in range(PACK)]
+        pieces = [slice(0, 256), slice(256, 384), slice(384, 512)]
+        quantize_w1(0)
+        for i, piece in enumerate(pieces):
+            nc.vector.tensor_copy(xg_w[:, piece], xw[:].indirect(offs_sb[:, piece.start // 16 : piece.stop // 16]))
+            acc = first_product(0, piece, "bank%d" % i)
+            if i < len(pieces) - 1:
+                nc.scalar.activation(h[0][:, piece], acc[:], ACT.Relu, scale=0.06)
+            else:
+                nc.vector.tensor_scalar(h[0][:, piece], acc[:], 0.06, 0.0, ALU.mult, ALU.max)
+        nc.scalar.activation(gate9[:], gate_raw[:], ACT.Copy, scale=9.0)
+        for t in range(1, PACK):
+            quantize_w1(t)
+            nc.scalar.activation(h[t][:], first_product(t, slice(0, S), "bank%d" % ((t + 2) % 4))[:], ACT.Relu, scale=0.06)
 
         w2_bf = keep.tile([P, PACK, P, PACK], BF16, name="w2_bf", align_bytes=64)
         w2_w = keep.tile([P, H], U32, name="w2_w", align_bytes=64)
         w2_s = keep.tile([P, H], U8, name="w2_s", align_bytes=64)
         turn4 = keep.tile([P, PACK], F32, name="turn4")
+
         y_w = keep.tile([P, V], U32, name="y_w", align_bytes=64)
         y_s = keep.tile([P, V], U8, name="y_s", align_bytes=64)
         out_rows = out_0.rearrange("(p t) v -> p t v", t=PACK)
         out_words = out_1[0].rearrange("p c r -> p (c r)").bitcast(I32)
+        u = keep.tile([P, NB, PACK, BW], F32, name="u")
 
-        def gathers(b):
-            v0, w = BLOCKS[b]
+        def look_up(t, v0, w):
             lst = slice(v0 // 16, (v0 + w) // 16)
-            ga = keep.tile([P, PACK, w], F32, name="ga%d" % b)
-            gb = keep.tile([P, PACK, w], F32, name="gb%d" % b)
-            gc = keep.tile([P, PACK, w], F32, name="gc%d" % b)
-            u = keep.tile([P, PACK, w], F32, name="u%d" % b)
+            parts = [keep.tile([P, w], F32, name="part%d_%d_%d" % (d, t, v0)) for d in range(3)]
+            nc.vector.tensor_copy(parts[0][:], h[t][:].indirect(cen_sb[:, lst]))
+            nc.vector.tensor_tensor(parts[1][:], h[t][:].indirect(pos1_sb[:, lst]), gate9[:, 0, v0 : v0 + w], ALU.mult)
+            nc.vector.tensor_tensor(parts[2][:], h[t][:].indirect(pos2_sb[:, lst]), gate9[:, 1, v0 : v0 + w], ALU.mult)
+            return parts
 
-            def mix(ts):
-                nc.vector.tensor_tensor(ga[:, ts, :], ga[:, ts, :], gb[:, ts, :], ALU.add)
+        def cast_w2(a):
+            deal(nc.scalar.copy, w2_bf, w2_raw, a * P // 2, (a + 1) * P // 2, 0)
 
-            def finish(ts):
-                nc.vector.scalar_tensor_tensor(u[:, ts, :], ga[:, ts, :], 9.0, gc[:, ts, :], ALU.mult, ALU.add)
+        def add_turned(target, part, b, d):
+            nc.tensor.matmul(target, part[:, b * BW : (b + 1) * BW], ident[:], start=(d == 0), stop=(d == 2), is_transpose=True)
 
-            for t in range(PACK):
-                nc.vector.tensor_tensor(ga[:, t, :], h[t][:].indirect(pos1_sb[:, lst]), gate_sb[:, 0, v0 : v0 + w], ALU.mult)
-                nc.vector.tensor_tensor(gb[:, t, :], h[t][:].indirect(pos2_sb[:, lst]), gate_sb[:, 1, v0 : v0 + w], ALU.mult)
-                if t == PACK - 1:
-                    mix(slice(0, PACK - 1))
-                nc.vector.tensor_copy(gc[:, t, :], h[t][:].indirect(cen_sb[:, lst]))
-            mix(slice(PACK - 1, PACK))
-            finish(slice(0, PACK - 1))
-            finish(slice(PACK - 1, PACK))
-            return u
+        def turn_back(turned_sb):
+            back = psum.tile([P, NB, BW], F32, name="back", tag="back", bufs=2)
+            for b in range(NB):
+                nc.tensor.transpose(back[:, b, :], turned_sb[:, b, :], ident[:])
+            return back
+
+        def sum_on_vector(t, b, parts):
+            nc.vector.tensor_tensor(parts[0][:], parts[0][:], parts[1][:], ALU.add)
+            nc.vector.tensor_tensor(u[:, b, t, :], parts[0][:], parts[2][:], ALU.add)
 
         def interleave(dst, src, scale):
             nc.scalar.activation(
-                dst[:].rearrange("p (c i) t -> p c t i", i=4),
-                src[:].rearrange("p t (c i) -> p c t i", i=4),
+                dst.rearrange("p (c i) t -> p c t i", i=4),
+                src.rearrange("p t (c i) -> p c t i", i=4),
                 ACT.Copy, scale=scale,
             )
 
-        def second(b, u):
-            v0, w = BLOCKS[b]
+        def second(b):
+            v0, w = b * BW, BW
             z_bf = keep.tile([P, w, PACK], BF16, name="z_bf%d" % b, align_bytes=64)
             z_w = keep.tile([P, w], U32, name="z_w%d" % b, align_bytes=64)
             z_s = keep.tile([P, w], U8, name="z_s%d" % b, align_bytes=64)
-            interleave(z_bf, u, 1.0 / 0.6)
+            interleave(z_bf[:], u[:, b, :, :], 1.0 / 0.6)
             nc.vector.quantize_mx(out=z_w[:].bitcast(FP8X4), scales=z_s[:], in_=z_bf[:].rearrange("p v t -> p (v t)"))
-            y = psum.tile([P, PACK, w], F32, name="y%d" % b)
+            y = psum.tile([P, PACK, w], F32, name="y%d" % b, tag="bank%d" % (b + 2))
             res = keep.tile([P, PACK, w], F32, name="res%d" % b)
             for t in range(PACK):
                 cols = slice(t * P, (t + 1) * P)
@@ -148,25 +170,53 @@ def tile_picked_zgcnii_relu_po_kernel(
                     rhs=z_w[:].bitcast(FP8X4), rhs_scale=z_s[:], start=True, stop=True,
                 )
             for t in range(PACK):
-                nc.vector.scalar_tensor_tensor(res[:, t, :], y[:, t, :], turn4[:, t : t + 1], u[:, t, :], ALU.mult, ALU.add)
+                nc.vector.scalar_tensor_tensor(res[:, t, :], y[:, t, :], turn4[:, t : t + 1], u[:, b, t, :], ALU.mult, ALU.add)
             nc.sync.dma_start(out_rows[:, :, v0 : v0 + w], res[:])
             res_bf = keep.tile([P, w, PACK], BF16, name="res_bf%d" % b, align_bytes=64)
-            interleave(res_bf, res, 1.0)
+            if b < NB - 1:
+                interleave(res_bf[:], res[:], 1.0)
+            else:
+                interleave(res_bf[:, 0:48, :], res[:, :, 0:48], 1.0)
+                nc.vector.tensor_copy(
+                    res_bf[:, 48:w, :].rearrange("p (c i) t -> p c t i", i=4),
+                    res[:, :, 48:w].rearrange("p t (c i) -> p c t i", i=4),
+                )
             nc.vector.quantize_mx(
                 out=y_w[:, v0 : v0 + w].bitcast(FP8X4), scales=y_s[:, v0 : v0 + w],
                 in_=res_bf[:].rearrange("p v t -> p (v t)"),
             )
             nc.sync.dma_start(out_words[:, v0 : v0 + w], y_w[:, v0 : v0 + w].bitcast(I32))
 
-        u0 = gathers(0)
-        deal(nc.scalar.copy, w2_bf, w2_raw, 0, P, 0)
-        nc.scalar.activation(turn4[:], turn_sb[:], ACT.Copy, scale=0.4)
+        nc.scalar.activation(turn4[:], turn_raw[:], ACT.Copy, scale=0.4)
+        turned_sb = [keep.tile([P, NB, P], F32, name="turned_sb%d" % t) for t in range(3)]
+        back = []
+        for t in range(2):
+            parts = look_up(t, 0, V)
+            turned = psum.tile([P, NB, P], F32, name="turned", tag="turned%d" % t)
+            for b in range(NB):
+                for d in range(3):
+                    add_turned(turned[:, b, :], parts[d], b, d)
+            cast_w2(t)
+            nc.scalar.copy(turned_sb[t][:], turned[:])
+            back.append(turn_back(turned_sb[t]))
+        nc.scalar.copy(u[:, :, 0, :], back[0][:])
+        parts = look_up(2, 0, V)
+        halves = [psum.tile([P, P], F32, name="half", tag="turned%d" % b) for b in range(NB)]
+        for d in range(3):
+            for b in range(NB):
+                add_turned(halves[b][:], parts[d], b, d)
+        for b in range(NB):
+            nc.scalar.copy(turned_sb[2][:, b, :], halves[b][:])
+        nc.scalar.copy(u[:, :, 1, :], back[1][:])
+        nc.scalar.copy(u[:, :, 2, :], turn_back(turned_sb[2])[:])
         nc.vector.quantize_mx(
             out=w2_w[:].bitcast(FP8X4), scales=w2_s[:], in_=w2_bf[:].rearrange("p t m j -> p (t m j)")
         )
-        second(0, u0)
-        u1 = gathers(1)
-        second(1, u1)
+        for b in range(NB):
+            for t in range(EARLY, PACK):
+                sum_on_vector(t, b, look_up(t, b * BW, BW))
+        for b in range(NB):
+            second(b)
         for q in range(4):
             queue = nc.sync if q % 2 == 0 else nc.scalar
             queue.dma_start(out_2[0][4 * q : 4 * q + 4, :].bitcast(I32), y_s[32 * q : 32 * q + 4, :].bitcast(I32))

@@ -23,10 +23,11 @@ NB = V // BW
 EARLY = 3
 
 
-def deal(engine_copy, grouped, raw, m0, m1, m_base):
+def deal(engine_copy, grouped, raw, pair):
+    ts = slice(2 * pair, 2 * pair + 2)
     engine_copy(
-        out=grouped[:, :, m0:m1, :].rearrange("p t m j -> p m j t"),
-        in_=raw[:].rearrange("p j (m t) -> p m j t", t=PACK)[:, m0 - m_base : m1 - m_base, :, :],
+        out=grouped[:, ts, :, :].rearrange("p t m j -> p m j t"),
+        in_=raw[:].rearrange("p j (m t) -> p m j t", t=PACK)[:, :, :, ts],
     )
 
 
@@ -76,8 +77,8 @@ def tile_picked_zgcnii_relu_po_kernel(
         w1_bf = keep.tile([P, PACK, P, PACK], BF16, name="w1_bf", align_bytes=64)
         w1_w = keep.tile([P, H], U32, name="w1_w", align_bytes=64)
         w1_s = keep.tile([P, H], U8, name="w1_s", align_bytes=64)
-        deal(nc.scalar.copy, w1_bf, w1_raw, 0, 44, 0)
-        deal(nc.vector.tensor_copy, w1_bf, w1_raw, 44, P, 0)
+        deal(nc.vector.tensor_copy, w1_bf, w1_raw, 0)
+        deal(nc.scalar.copy, w1_bf, w1_raw, 1)
         gate9 = keep.tile([P, 2, V], F32, name="gate9")
 
         def quantize_w1(t):
@@ -132,7 +133,7 @@ def tile_picked_zgcnii_relu_po_kernel(
             return parts
 
         def cast_w2(a):
-            deal(nc.scalar.copy, w2_bf, w2_raw, a * P // 2, (a + 1) * P // 2, 0)
+            deal(nc.scalar.copy, w2_bf, w2_raw, a)
 
         def add_turned(target, part, b, d):
             nc.tensor.matmul(target, part[:, b * BW : (b + 1) * BW], ident[:], start=(d == 0), stop=(d == 2), is_transpose=True)
@@ -149,8 +150,8 @@ def tile_picked_zgcnii_relu_po_kernel(
 
         def interleave(dst, src, scale):
             nc.scalar.activation(
-                dst.rearrange("p (c i) t -> p c t i", i=4),
-                src.rearrange("p t (c i) -> p c t i", i=4),
+                dst.rearrange("p (c i) t -> p c t i", i=2),
+                src.rearrange("p t (c i) -> p c t i", i=2),
                 ACT.Copy, scale=scale,
             )
 
@@ -178,8 +179,8 @@ def tile_picked_zgcnii_relu_po_kernel(
             else:
                 interleave(res_bf[:, 0:48, :], res[:, :, 0:48], 1.0)
                 nc.vector.tensor_copy(
-                    res_bf[:, 48:w, :].rearrange("p (c i) t -> p c t i", i=4),
-                    res[:, :, 48:w].rearrange("p t (c i) -> p c t i", i=4),
+                    res_bf[:, 48:w, :].rearrange("p (c i) t -> p c t i", i=2),
+                    res[:, :, 48:w].rearrange("p t (c i) -> p c t i", i=2),
                 )
             nc.vector.quantize_mx(
                 out=y_w[:, v0 : v0 + w].bitcast(FP8X4), scales=y_s[:, v0 : v0 + w],

@@ -18,17 +18,31 @@ ACT = mybir.ActivationFunctionType
 
 P = 128
 PACK = 4
-BW = 128
-NB = V // BW
-EARLY = 3
+QUADRANTS = 4
+LIST_ROWS = 16
+TERMS = 3
+BLOCK = 128
+BLOCKS = V // BLOCK
+
+H_SCALE = 0.06
+GATE_SCALE = 9.0
+Z_SCALE = 1.0 / 0.6
+TURN_SCALE = 0.4
+
+H0_PIECES = [slice(0, 256), slice(256, 384), slice(384, 512)]
+SCALAR_SHARE = 48
 
 
-def deal(engine_copy, grouped, raw, pair):
+def deal(copy, grouped, raw, pair):
     ts = slice(2 * pair, 2 * pair + 2)
-    engine_copy(
+    copy(
         out=grouped[:, ts, :, :].rearrange("p t m j -> p m j t"),
         in_=raw[:].rearrange("p j (m t) -> p m j t", t=PACK)[:, :, :, ts],
     )
+
+
+def side_by_side(packed, row_tiles):
+    return packed.rearrange("p (c i) t -> p c t i", i=2), row_tiles.rearrange("p t (c i) -> p c t i", i=2)
 
 
 def tile_picked_zgcnii_relu_po_kernel(
@@ -39,26 +53,28 @@ def tile_picked_zgcnii_relu_po_kernel(
         keep = ctx.enter_context(tc.tile_pool(name="keep", bufs=1))
         psum = ctx.enter_context(tc.psum_pool(name="psum", bufs=1))
 
-        offs_sb = keep.tile([P, S // 16], U16, name="offs_sb")
-        cen_sb = keep.tile([P, V // 16], U16, name="cen_sb")
-        pos1_sb = keep.tile([P, V // 16], U16, name="pos1_sb")
-        pos2_sb = keep.tile([P, V // 16], U16, name="pos2_sb")
-        xw = keep.tile([P, T], U32, name="xw")
-        xs = keep.tile([P, T], U8, name="xs")
+        offs_sb = keep.tile([P, S // LIST_ROWS], U16, name="offs_sb")
+        cen_sb = keep.tile([P, V // LIST_ROWS], U16, name="cen_sb")
+        pos1_sb = keep.tile([P, V // LIST_ROWS], U16, name="pos1_sb")
+        pos2_sb = keep.tile([P, V // LIST_ROWS], U16, name="pos2_sb")
+        x_word_table = keep.tile([P, T], U32, name="x_word_table")
+        x_scale_table = keep.tile([P, T], U8, name="x_scale_table")
         w1_raw = keep.tile([P, PACK, H], F32, name="w1_raw")
-        w2_raw = keep.tile([P, PACK, H], F32, name="w2_raw")
+        w2_raw = keep.tile([P, PACK, H], F32, name="w2_raw", tag="stage")
         turn_raw = keep.tile([P, PACK], F32, name="turn_raw")
-        xs_rows = keep.tile([P, T], U8, name="xs_rows")
+        x_scale_rows = keep.tile([P, T], U8, name="x_scale_rows")
         gate_raw = keep.tile([P, 2, V], F32, name="gate_raw")
         ident = keep.tile([P, P], F32, name="ident")
 
-        quadrants = [slice(32 * q, 32 * q + 4) for q in range(4)]
-        for q in range(4):
-            queue = nc.scalar if q < 2 else nc.sync
-            queue.dma_start(xs_rows[quadrants[q], :].bitcast(I32), x_scales[0][4 * q : 4 * q + 4, :].bitcast(I32))
+        scale_partitions = [slice(32 * q, 32 * q + 4) for q in range(QUADRANTS)]
+        for q in range(QUADRANTS):
+            queue = nc.scalar if q < QUADRANTS // 2 else nc.sync
+            queue.dma_start(
+                x_scale_rows[scale_partitions[q], :].bitcast(I32), x_scales[0][4 * q : 4 * q + 4, :].bitcast(I32)
+            )
         nc.sync.dma_start(offs_sb[:], offs)
         nc.sync.dma_start(w1_raw[:], w1.rearrange("(p j) c -> p j c", j=PACK))
-        nc.sync.dma_start(xw[:].bitcast(I32), x_words[0].rearrange("p c r -> p (c r)").bitcast(I32))
+        nc.sync.dma_start(x_word_table[:].bitcast(I32), x_words[0].rearrange("p c r -> p (c r)").bitcast(I32))
         nc.sync.dma_start(cen_sb[:], cen)
         nc.sync.dma_start(pos1_sb[:], pos1)
         nc.sync.dma_start(pos2_sb[:], pos2)
@@ -67,157 +83,164 @@ def tile_picked_zgcnii_relu_po_kernel(
         nc.sync.dma_start(w2_raw[:], w2.rearrange("(p j) c -> p j c", j=PACK))
         make_identity(nc, ident[:])
 
-        nc.vector.memset(xs[:].bitcast(I32), 0)
-        for q in range(4):
-            nc.vector.tensor_copy(xs[quadrants[q], :].bitcast(I32), xs_rows[quadrants[q], :].bitcast(I32))
-        xg_w = keep.tile([P, S], U32, name="xg_w", align_bytes=64)
-        xg_s = keep.tile([P, S], U8, name="xg_s", align_bytes=64)
-        nc.vector.tensor_copy(xg_s[:], xs[:].indirect(offs_sb[:]))
+        nc.vector.memset(x_scale_table[:].bitcast(I32), 0)
+        for q in range(QUADRANTS):
+            nc.vector.tensor_copy(
+                x_scale_table[scale_partitions[q], :].bitcast(I32), x_scale_rows[scale_partitions[q], :].bitcast(I32)
+            )
+        picked_words = keep.tile([P, S], U32, name="picked_words", align_bytes=64)
+        picked_scales = keep.tile([P, S], U8, name="picked_scales", align_bytes=64)
+        nc.vector.tensor_copy(picked_scales[:], x_scale_table[:].indirect(offs_sb[:]))
 
         w1_bf = keep.tile([P, PACK, P, PACK], BF16, name="w1_bf", align_bytes=64)
-        w1_w = keep.tile([P, H], U32, name="w1_w", align_bytes=64)
-        w1_s = keep.tile([P, H], U8, name="w1_s", align_bytes=64)
+        w1_words = keep.tile([P, H], U32, name="w1_words", align_bytes=64)
+        w1_scales = keep.tile([P, H], U8, name="w1_scales", align_bytes=64)
         deal(nc.vector.tensor_copy, w1_bf, w1_raw, 0)
         deal(nc.scalar.copy, w1_bf, w1_raw, 1)
-        gate9 = keep.tile([P, 2, V], F32, name="gate9")
+        gate_scaled = keep.tile([P, 2, V], F32, name="gate_scaled")
 
         def quantize_w1(t):
             cols = slice(t * P, (t + 1) * P)
             nc.vector.quantize_mx(
-                out=w1_w[:, cols].bitcast(FP8X4),
-                scales=w1_s[:, cols],
+                out=w1_words[:, cols].bitcast(FP8X4),
+                scales=w1_scales[:, cols],
                 in_=w1_bf[:, t, :, :].rearrange("p m j -> p (m j)"),
             )
 
-        def first_product(t, entries, tag):
+        def first_product(t, entries, bank):
             cols = slice(t * P, (t + 1) * P)
-            acc = psum.tile([P, entries.stop - entries.start], F32, name="h_acc", tag=tag)
+            acc = psum.tile([P, entries.stop - entries.start], F32, name="h_acc", tag="bank%d" % bank)
             nc.tensor.matmul_mx(
-                out=acc[:], lhsT=w1_w[:, cols].bitcast(FP8X4), lhsT_scale=w1_s[:, cols],
-                rhs=xg_w[:, entries].bitcast(FP8X4), rhs_scale=xg_s[:, entries], start=True, stop=True,
+                out=acc[:],
+                lhsT=w1_words[:, cols].bitcast(FP8X4),
+                lhsT_scale=w1_scales[:, cols],
+                rhs=picked_words[:, entries].bitcast(FP8X4),
+                rhs_scale=picked_scales[:, entries],
+                start=True,
+                stop=True,
             )
             return acc
 
         h = [keep.tile([P, S], F32, name="h%d" % t) for t in range(PACK)]
-        pieces = [slice(0, 256), slice(256, 384), slice(384, 512)]
         quantize_w1(0)
-        for i, piece in enumerate(pieces):
-            nc.vector.tensor_copy(xg_w[:, piece], xw[:].indirect(offs_sb[:, piece.start // 16 : piece.stop // 16]))
-            acc = first_product(0, piece, "bank%d" % i)
-            if i < len(pieces) - 1:
-                nc.scalar.activation(h[0][:, piece], acc[:], ACT.Relu, scale=0.06)
+        for i, piece in enumerate(H0_PIECES):
+            entries = offs_sb[:, piece.start // LIST_ROWS : piece.stop // LIST_ROWS]
+            nc.vector.tensor_copy(picked_words[:, piece], x_word_table[:].indirect(entries))
+            acc = first_product(0, piece, i)
+            if i < len(H0_PIECES) - 1:
+                nc.scalar.activation(h[0][:, piece], acc[:], ACT.Relu, scale=H_SCALE)
             else:
-                nc.vector.tensor_scalar(h[0][:, piece], acc[:], 0.06, 0.0, ALU.mult, ALU.max)
-        nc.scalar.activation(gate9[:], gate_raw[:], ACT.Copy, scale=9.0)
+                nc.vector.tensor_scalar(h[0][:, piece], acc[:], H_SCALE, 0.0, ALU.mult, ALU.max)
+        nc.scalar.activation(gate_scaled[:], gate_raw[:], ACT.Copy, scale=GATE_SCALE)
         for t in range(1, PACK):
             quantize_w1(t)
-            nc.scalar.activation(h[t][:], first_product(t, slice(0, S), "bank%d" % ((t + 2) % 4))[:], ACT.Relu, scale=0.06)
+            acc = first_product(t, slice(0, S), (t + 2) % 4)
+            nc.scalar.activation(h[t][:], acc[:], ACT.Relu, scale=H_SCALE)
 
         w2_bf = keep.tile([P, PACK, P, PACK], BF16, name="w2_bf", align_bytes=64)
-        w2_w = keep.tile([P, H], U32, name="w2_w", align_bytes=64)
-        w2_s = keep.tile([P, H], U8, name="w2_s", align_bytes=64)
-        turn4 = keep.tile([P, PACK], F32, name="turn4")
+        w2_words = keep.tile([P, H], U32, name="w2_words", align_bytes=64)
+        w2_scales = keep.tile([P, H], U8, name="w2_scales", align_bytes=64)
+        turn_scaled = keep.tile([P, PACK], F32, name="turn_scaled")
+        out_words = keep.tile([P, V], U32, name="out_words", align_bytes=64)
+        out_scales = keep.tile([P, V], U8, name="out_scales", align_bytes=64)
+        out_0_rows = out_0.rearrange("(p t) v -> p t v", t=PACK)
+        out_1_words = out_1[0].rearrange("p c r -> p (c r)").bitcast(I32)
+        u = [keep.tile([P, PACK, BLOCK], F32, name="u%d" % b) for b in range(BLOCKS)]
+        targets = [slice(b * BLOCK, (b + 1) * BLOCK) for b in range(BLOCKS)]
 
-        y_w = keep.tile([P, V], U32, name="y_w", align_bytes=64)
-        y_s = keep.tile([P, V], U8, name="y_s", align_bytes=64)
-        out_rows = out_0.rearrange("(p t) v -> p t v", t=PACK)
-        out_words = out_1[0].rearrange("p c r -> p (c r)").bitcast(I32)
-        u = keep.tile([P, NB, PACK, BW], F32, name="u")
+        def look_up(t):
+            terms = [keep.tile([P, V], F32, name="term%d_%d" % (d, t)) for d in range(TERMS)]
+            nc.vector.tensor_copy(terms[0][:], h[t][:].indirect(cen_sb[:]))
+            nc.vector.tensor_tensor(terms[1][:], h[t][:].indirect(pos1_sb[:]), gate_scaled[:, 0, :], ALU.mult)
+            nc.vector.tensor_tensor(terms[2][:], h[t][:].indirect(pos2_sb[:]), gate_scaled[:, 1, :], ALU.mult)
+            return terms
 
-        def look_up(t, v0, w):
-            lst = slice(v0 // 16, (v0 + w) // 16)
-            parts = [keep.tile([P, w], F32, name="part%d_%d_%d" % (d, t, v0)) for d in range(3)]
-            nc.vector.tensor_copy(parts[0][:], h[t][:].indirect(cen_sb[:, lst]))
-            nc.vector.tensor_tensor(parts[1][:], h[t][:].indirect(pos1_sb[:, lst]), gate9[:, 0, v0 : v0 + w], ALU.mult)
-            nc.vector.tensor_tensor(parts[2][:], h[t][:].indirect(pos2_sb[:, lst]), gate9[:, 1, v0 : v0 + w], ALU.mult)
-            return parts
-
-        def cast_w2(a):
-            deal(nc.scalar.copy, w2_bf, w2_raw, a)
-
-        def add_turned(target, part, b, d):
-            nc.tensor.matmul(target, part[:, b * BW : (b + 1) * BW], ident[:], start=(d == 0), stop=(d == 2), is_transpose=True)
-
-        def turn_back(turned_sb):
-            back = psum.tile([P, NB, BW], F32, name="back", tag="back", bufs=2)
-            for b in range(NB):
-                nc.tensor.transpose(back[:, b, :], turned_sb[:, b, :], ident[:])
-            return back
-
-        def sum_on_vector(t, b, parts):
-            nc.vector.tensor_tensor(parts[0][:], parts[0][:], parts[1][:], ALU.add)
-            nc.vector.tensor_tensor(u[:, b, t, :], parts[0][:], parts[2][:], ALU.add)
-
-        def interleave(dst, src, scale):
-            nc.scalar.activation(
-                dst.rearrange("p (c i) t -> p c t i", i=2),
-                src.rearrange("p t (c i) -> p c t i", i=2),
-                ACT.Copy, scale=scale,
+        def add_turned(total, terms, b, d):
+            nc.tensor.matmul(
+                total, terms[d][:, targets[b]], ident[:], start=(d == 0), stop=(d == TERMS - 1), is_transpose=True
             )
 
-        def second(b):
-            v0, w = b * BW, BW
-            z_bf = keep.tile([P, w, PACK], BF16, name="z_bf%d" % b, align_bytes=64)
-            z_w = keep.tile([P, w], U32, name="z_w%d" % b, align_bytes=64)
-            z_s = keep.tile([P, w], U8, name="z_s%d" % b, align_bytes=64)
-            interleave(z_bf[:], u[:, b, :, :], 1.0 / 0.6)
-            nc.vector.quantize_mx(out=z_w[:].bitcast(FP8X4), scales=z_s[:], in_=z_bf[:].rearrange("p v t -> p (v t)"))
-            y = psum.tile([P, PACK, w], F32, name="y%d" % b, tag="bank%d" % (b + 2))
-            res = keep.tile([P, PACK, w], F32, name="res%d" % b)
+        def turn_back(b):
+            back = psum.tile([P, PACK - 1, BLOCK], F32, name="back", tag="back%d" % b)
+            for t in range(PACK - 1):
+                nc.tensor.transpose(back[:, t, :], turned_sb[:, t, b, :], ident[:])
+            nc.scalar.copy(u[b][:, 0 : PACK - 1, :], back[:])
+
+        def finish_block(b):
+            z_bf = keep.tile([P, BLOCK, PACK], BF16, name="z_bf%d" % b, align_bytes=64)
+            z_words = keep.tile([P, BLOCK], U32, name="z_words%d" % b, align_bytes=64)
+            z_scales = keep.tile([P, BLOCK], U8, name="z_scales%d" % b, align_bytes=64)
+            nc.scalar.activation(*side_by_side(z_bf[:], u[b][:]), ACT.Copy, scale=Z_SCALE)
+            nc.vector.quantize_mx(
+                out=z_words[:].bitcast(FP8X4), scales=z_scales[:], in_=z_bf[:].rearrange("p v t -> p (v t)")
+            )
+            y = psum.tile([P, PACK, BLOCK], F32, name="y%d" % b, tag="bank%d" % (b + 2))
+            result = keep.tile([P, PACK, BLOCK], F32, name="result%d" % b)
             for t in range(PACK):
                 cols = slice(t * P, (t + 1) * P)
                 nc.tensor.matmul_mx(
-                    out=y[:, t, :], lhsT=w2_w[:, cols].bitcast(FP8X4), lhsT_scale=w2_s[:, cols],
-                    rhs=z_w[:].bitcast(FP8X4), rhs_scale=z_s[:], start=True, stop=True,
+                    out=y[:, t, :],
+                    lhsT=w2_words[:, cols].bitcast(FP8X4),
+                    lhsT_scale=w2_scales[:, cols],
+                    rhs=z_words[:].bitcast(FP8X4),
+                    rhs_scale=z_scales[:],
+                    start=True,
+                    stop=True,
                 )
             for t in range(PACK):
-                nc.vector.scalar_tensor_tensor(res[:, t, :], y[:, t, :], turn4[:, t : t + 1], u[:, b, t, :], ALU.mult, ALU.add)
-            nc.sync.dma_start(out_rows[:, :, v0 : v0 + w], res[:])
-            res_bf = keep.tile([P, w, PACK], BF16, name="res_bf%d" % b, align_bytes=64)
-            if b < NB - 1:
-                interleave(res_bf[:], res[:], 1.0)
-            else:
-                interleave(res_bf[:, 0:48, :], res[:, :, 0:48], 1.0)
-                nc.vector.tensor_copy(
-                    res_bf[:, 48:w, :].rearrange("p (c i) t -> p c t i", i=2),
-                    res[:, :, 48:w].rearrange("p t (c i) -> p c t i", i=2),
+                nc.vector.scalar_tensor_tensor(
+                    result[:, t, :], y[:, t, :], turn_scaled[:, t : t + 1], u[b][:, t, :], ALU.mult, ALU.add
                 )
-            nc.vector.quantize_mx(
-                out=y_w[:, v0 : v0 + w].bitcast(FP8X4), scales=y_s[:, v0 : v0 + w],
-                in_=res_bf[:].rearrange("p v t -> p (v t)"),
-            )
-            nc.sync.dma_start(out_words[:, v0 : v0 + w], y_w[:, v0 : v0 + w].bitcast(I32))
+            nc.sync.dma_start(out_0_rows[:, :, targets[b]], result[:])
 
-        nc.scalar.activation(turn4[:], turn_raw[:], ACT.Copy, scale=0.4)
-        turned_sb = [keep.tile([P, NB, P], F32, name="turned_sb%d" % t) for t in range(3)]
-        back = []
-        for t in range(2):
-            parts = look_up(t, 0, V)
-            turned = psum.tile([P, NB, P], F32, name="turned", tag="turned%d" % t)
-            for b in range(NB):
-                for d in range(3):
-                    add_turned(turned[:, b, :], parts[d], b, d)
-            cast_w2(t)
-            nc.scalar.copy(turned_sb[t][:], turned[:])
-            back.append(turn_back(turned_sb[t]))
-        nc.scalar.copy(u[:, :, 0, :], back[0][:])
-        parts = look_up(2, 0, V)
-        halves = [psum.tile([P, P], F32, name="half", tag="turned%d" % b) for b in range(NB)]
-        for d in range(3):
-            for b in range(NB):
-                add_turned(halves[b][:], parts[d], b, d)
-        for b in range(NB):
-            nc.scalar.copy(turned_sb[2][:, b, :], halves[b][:])
-        nc.scalar.copy(u[:, :, 1, :], back[1][:])
-        nc.scalar.copy(u[:, :, 2, :], turn_back(turned_sb[2])[:])
+            result_bf = keep.tile([P, BLOCK, PACK], BF16, name="result_bf%d" % b, align_bytes=64)
+            if b < BLOCKS - 1:
+                nc.scalar.activation(*side_by_side(result_bf[:], result[:]), ACT.Copy, scale=1.0)
+            else:
+                first, rest = slice(0, SCALAR_SHARE), slice(SCALAR_SHARE, BLOCK)
+                nc.scalar.activation(*side_by_side(result_bf[:, first, :], result[:, :, first]), ACT.Copy, scale=1.0)
+                nc.vector.tensor_copy(*side_by_side(result_bf[:, rest, :], result[:, :, rest]))
+            nc.vector.quantize_mx(
+                out=out_words[:, targets[b]].bitcast(FP8X4),
+                scales=out_scales[:, targets[b]],
+                in_=result_bf[:].rearrange("p v t -> p (v t)"),
+            )
+            nc.sync.dma_start(out_1_words[:, targets[b]], out_words[:, targets[b]].bitcast(I32))
+
+        nc.scalar.activation(turn_scaled[:], turn_raw[:], ACT.Copy, scale=TURN_SCALE)
+        for pair in range(PACK // 2):
+            deal(nc.scalar.copy, w2_bf, w2_raw, pair)
+
+        turned_sb = keep.tile([P, PACK - 1, BLOCKS, P], F32, name="turned_sb", tag="stage")
+        for t in range(PACK - 2):
+            terms = look_up(t)
+            turned = psum.tile([P, BLOCKS, P], F32, name="turned", tag="turned%d" % t)
+            for b in range(BLOCKS):
+                for d in range(TERMS):
+                    add_turned(turned[:, b, :], terms, b, d)
+            nc.scalar.copy(turned_sb[:, t, :, :], turned[:])
+        terms = look_up(PACK - 2)
+        turned_by_block = [psum.tile([P, P], F32, name="turned_block", tag="bank%d" % b) for b in range(BLOCKS)]
+        for d in range(TERMS):
+            for b in range(BLOCKS):
+                add_turned(turned_by_block[b][:], terms, b, d)
+        for b in range(BLOCKS):
+            nc.scalar.copy(turned_sb[:, PACK - 2, b, :], turned_by_block[b][:])
+        turn_back(0)
         nc.vector.quantize_mx(
-            out=w2_w[:].bitcast(FP8X4), scales=w2_s[:], in_=w2_bf[:].rearrange("p t m j -> p (t m j)")
+            out=w2_words[:].bitcast(FP8X4), scales=w2_scales[:], in_=w2_bf[:].rearrange("p t m j -> p (t m j)")
         )
-        for b in range(NB):
-            for t in range(EARLY, PACK):
-                sum_on_vector(t, b, look_up(t, b * BW, BW))
-        for b in range(NB):
-            second(b)
-        for q in range(4):
+
+        terms = look_up(PACK - 1)
+        nc.vector.tensor_tensor(terms[0][:], terms[0][:], terms[1][:], ALU.add)
+        for b in range(BLOCKS):
+            nc.vector.tensor_tensor(u[b][:, PACK - 1, :], terms[0][:, targets[b]], terms[2][:, targets[b]], ALU.add)
+
+        finish_block(0)
+        turn_back(1)
+        finish_block(1)
+        for q in range(QUADRANTS):
             queue = nc.sync if q % 2 == 0 else nc.scalar
-            queue.dma_start(out_2[0][4 * q : 4 * q + 4, :].bitcast(I32), y_s[32 * q : 32 * q + 4, :].bitcast(I32))
+            queue.dma_start(
+                out_2[0][4 * q : 4 * q + 4, :].bitcast(I32), out_scales[scale_partitions[q], :].bitcast(I32)
+            )

@@ -28,16 +28,16 @@ H_SCALE = 0.06
 GATE_SCALE = 9.0
 Z_SCALE = 1.0 / 0.6
 TURN_SCALE = 0.4
+NEAR_SCALE = 0.54
 
 H0_PIECES = [slice(0, 256), slice(256, 384), slice(384, 512)]
 SCALAR_SHARE = 48
 
 
 def deal(copy, grouped, raw, pair):
-    ts = slice(2 * pair, 2 * pair + 2)
     copy(
-        out=grouped[:, ts, :, :].rearrange("p t m j -> p m j t"),
-        in_=raw[:].rearrange("p j (m t) -> p m j t", t=PACK)[:, :, :, ts],
+        out=grouped.rearrange("p i m j -> p m j i"),
+        in_=raw[:].rearrange("p j (m t) -> p m j t", t=PACK)[:, :, :, 2 * pair : 2 * pair + 2],
     )
 
 
@@ -59,7 +59,7 @@ def tile_picked_zgcnii_relu_po_kernel(
         pos2_sb = keep.tile([P, V // LIST_ROWS], U16, name="pos2_sb")
         x_word_table = keep.tile([P, T], U32, name="x_word_table")
         x_scale_table = keep.tile([P, T], U8, name="x_scale_table")
-        w1_raw = keep.tile([P, PACK, H], F32, name="w1_raw")
+        w1_raw = [keep.tile([P, PACK, H // 2], F32, name="w1_raw%d" % half) for half in range(2)]
         w2_raw = keep.tile([P, PACK, H], F32, name="w2_raw", tag="stage")
         turn_raw = keep.tile([P, PACK], F32, name="turn_raw")
         x_scale_rows = keep.tile([P, T], U8, name="x_scale_rows")
@@ -73,14 +73,16 @@ def tile_picked_zgcnii_relu_po_kernel(
                 x_scale_rows[scale_partitions[q], :].bitcast(I32), x_scales[0][4 * q : 4 * q + 4, :].bitcast(I32)
             )
         nc.sync.dma_start(offs_sb[:], offs)
-        nc.sync.dma_start(w1_raw[:], w1.rearrange("(p j) c -> p j c", j=PACK))
+        w1_rows = w1.rearrange("(p j) c -> p j c", j=PACK)
+        nc.sync.dma_start(w1_raw[0][:], w1_rows[:, :, 0 : H // 2])
         nc.sync.dma_start(x_word_table[:].bitcast(I32), x_words[0].rearrange("p c r -> p (c r)").bitcast(I32))
+        nc.sync.dma_start(w1_raw[1][:], w1_rows[:, :, H // 2 : H])
         nc.sync.dma_start(cen_sb[:], cen)
+        nc.sync.dma_start(gate_raw[:], gate.rearrange("d p v -> p d v"))
         nc.sync.dma_start(pos1_sb[:], pos1)
         nc.sync.dma_start(pos2_sb[:], pos2)
-        nc.sync.dma_start(gate_raw[:], gate.rearrange("d p v -> p d v"))
-        nc.sync.dma_start(turn_raw[:], turn.rearrange("(p t) o -> p (t o)", t=PACK))
         nc.sync.dma_start(w2_raw[:], w2.rearrange("(p j) c -> p j c", j=PACK))
+        nc.sync.dma_start(turn_raw[:], turn.rearrange("(p t) o -> p (t o)", t=PACK))
         make_identity(nc, ident[:])
 
         nc.vector.memset(x_scale_table[:].bitcast(I32), 0)
@@ -88,23 +90,25 @@ def tile_picked_zgcnii_relu_po_kernel(
             nc.vector.tensor_copy(
                 x_scale_table[scale_partitions[q], :].bitcast(I32), x_scale_rows[scale_partitions[q], :].bitcast(I32)
             )
+        centre_share = keep.tile([P, V], F32, name="centre_share")
+        ones = keep.tile([P, V], F32, name="ones")
+        nc.vector.memset(ones[:], 1.0)
+        nc.vector.tensor_scalar_mul(centre_share[:], ones[:], 1.0 / GATE_SCALE)
         picked_words = keep.tile([P, S], U32, name="picked_words", align_bytes=64)
         picked_scales = keep.tile([P, S], U8, name="picked_scales", align_bytes=64)
         nc.vector.tensor_copy(picked_scales[:], x_scale_table[:].indirect(offs_sb[:]))
 
-        w1_bf = keep.tile([P, PACK, P, PACK], BF16, name="w1_bf", align_bytes=64)
-        w1_words = keep.tile([P, H], U32, name="w1_words", align_bytes=64)
+        w1_half_bf = [keep.tile([P, 2, P // 2, PACK], BF16, name="w1_half_bf%d" % i, tag=tag, align_bytes=64) for i, tag in enumerate(["w1_first_bf", "term0_0"])]
+        w1_rest_bf = keep.tile([P, 2, P, PACK], BF16, name="w1_rest_bf", tag="term2_0", align_bytes=64)
+        w1_words = keep.tile([P, H], U32, name="w1_words", tag="weights", align_bytes=64)
         w1_scales = keep.tile([P, H], U8, name="w1_scales", align_bytes=64)
-        deal(nc.vector.tensor_copy, w1_bf, w1_raw, 0)
-        deal(nc.scalar.copy, w1_bf, w1_raw, 1)
         gate_scaled = keep.tile([P, 2, V], F32, name="gate_scaled")
 
-        def quantize_w1(t):
-            cols = slice(t * P, (t + 1) * P)
+        def quantize_w1(cols, grouped):
             nc.vector.quantize_mx(
                 out=w1_words[:, cols].bitcast(FP8X4),
                 scales=w1_scales[:, cols],
-                in_=w1_bf[:, t, :, :].rearrange("p m j -> p (m j)"),
+                in_=grouped[:].rearrange("p i m j -> p (i m j)"),
             )
 
         def first_product(t, entries, bank):
@@ -122,22 +126,24 @@ def tile_picked_zgcnii_relu_po_kernel(
             return acc
 
         h = [keep.tile([P, S], F32, name="h%d" % t) for t in range(PACK)]
-        quantize_w1(0)
+        deal(nc.vector.tensor_copy, w1_half_bf[0][:], w1_raw[0], 0)
+        deal(nc.scalar.copy, w1_rest_bf[:, :, 0 : P // 2, :], w1_raw[0], 1)
+        quantize_w1(slice(0, P), w1_half_bf[0])
         for i, piece in enumerate(H0_PIECES):
             entries = offs_sb[:, piece.start // LIST_ROWS : piece.stop // LIST_ROWS]
             nc.vector.tensor_copy(picked_words[:, piece], x_word_table[:].indirect(entries))
             acc = first_product(0, piece, i)
-            if i < len(H0_PIECES) - 1:
-                nc.scalar.activation(h[0][:, piece], acc[:], ACT.Relu, scale=H_SCALE)
-            else:
-                nc.vector.tensor_scalar(h[0][:, piece], acc[:], H_SCALE, 0.0, ALU.mult, ALU.max)
-        nc.scalar.activation(gate_scaled[:], gate_raw[:], ACT.Copy, scale=GATE_SCALE)
+            nc.scalar.activation(h[0][:, piece], acc[:], ACT.Relu, scale=NEAR_SCALE)
+        deal(nc.vector.tensor_copy, w1_half_bf[1][:], w1_raw[1], 0)
+        deal(nc.scalar.copy, w1_rest_bf[:, :, P // 2 : P, :], w1_raw[1], 1)
+        quantize_w1(slice(P, 2 * P), w1_half_bf[1])
         for t in range(1, PACK):
-            quantize_w1(t)
+            if t == 2:
+                quantize_w1(slice(2 * P, H), w1_rest_bf)
             acc = first_product(t, slice(0, S), (t + 2) % 4)
-            nc.scalar.activation(h[t][:], acc[:], ACT.Relu, scale=H_SCALE)
+            nc.scalar.activation(h[t][:], acc[:], ACT.Relu, scale=H_SCALE if t == PACK - 1 else NEAR_SCALE)
 
-        w2_bf = keep.tile([P, PACK, P, PACK], BF16, name="w2_bf", align_bytes=64)
+        w2_bf = keep.tile([P, PACK, P, PACK], BF16, name="w2_bf", tag="weights", align_bytes=64)
         w2_words = keep.tile([P, H], U32, name="w2_words", align_bytes=64)
         w2_scales = keep.tile([P, H], U8, name="w2_scales", align_bytes=64)
         turn_scaled = keep.tile([P, PACK], F32, name="turn_scaled")
@@ -149,10 +155,10 @@ def tile_picked_zgcnii_relu_po_kernel(
         targets = [slice(b * BLOCK, (b + 1) * BLOCK) for b in range(BLOCKS)]
 
         def look_up(t):
-            terms = [keep.tile([P, V], F32, name="term%d_%d" % (d, t)) for d in range(TERMS)]
-            nc.vector.tensor_copy(terms[0][:], h[t][:].indirect(cen_sb[:]))
-            nc.vector.tensor_tensor(terms[1][:], h[t][:].indirect(pos1_sb[:]), gate_scaled[:, 0, :], ALU.mult)
-            nc.vector.tensor_tensor(terms[2][:], h[t][:].indirect(pos2_sb[:]), gate_scaled[:, 1, :], ALU.mult)
+            terms = [keep.tile([P, V], F32, name="term%d_%d" % (d, t), align_bytes=64) for d in range(TERMS)]
+            nc.vector.tensor_tensor(terms[0][:], h[t][:].indirect(cen_sb[:]), centre_share[:], ALU.mult)
+            nc.vector.tensor_tensor(terms[1][:], h[t][:].indirect(pos1_sb[:]), gate_raw[:, 0, :], ALU.mult)
+            nc.vector.tensor_tensor(terms[2][:], h[t][:].indirect(pos2_sb[:]), gate_raw[:, 1, :], ALU.mult)
             return terms
 
         def add_turned(total, terms, b, d):
@@ -160,11 +166,11 @@ def tile_picked_zgcnii_relu_po_kernel(
                 total, terms[d][:, targets[b]], ident[:], start=(d == 0), stop=(d == TERMS - 1), is_transpose=True
             )
 
-        def turn_back(b):
-            back = psum.tile([P, PACK - 1, BLOCK], F32, name="back", tag="back%d" % b)
-            for t in range(PACK - 1):
-                nc.tensor.transpose(back[:, t, :], turned_sb[:, t, b, :], ident[:])
-            nc.scalar.copy(u[b][:, 0 : PACK - 1, :], back[:])
+        def turn_back(b, tiles, tag):
+            back = psum.tile([P, tiles.stop - tiles.start, BLOCK], F32, name="back", tag=tag)
+            for t in range(tiles.start, tiles.stop):
+                nc.tensor.transpose(back[:, t - tiles.start, :], turned_sb[:, t, b, :], ident[:])
+            nc.scalar.copy(u[b][:, tiles, :], back[:])
 
         def finish_block(b):
             z_bf = keep.tile([P, BLOCK, PACK], BF16, name="z_bf%d" % b, align_bytes=64)
@@ -207,37 +213,53 @@ def tile_picked_zgcnii_relu_po_kernel(
             )
             nc.sync.dma_start(out_1_words[:, targets[b]], out_words[:, targets[b]].bitcast(I32))
 
+        nc.scalar.activation(gate_scaled[:], gate_raw[:], ACT.Copy, scale=GATE_SCALE)
         nc.scalar.activation(turn_scaled[:], turn_raw[:], ACT.Copy, scale=TURN_SCALE)
         for pair in range(PACK // 2):
-            deal(nc.scalar.copy, w2_bf, w2_raw, pair)
+            deal(nc.scalar.copy, w2_bf[:, 2 * pair : 2 * pair + 2, :, :], w2_raw, pair)
 
         turned_sb = keep.tile([P, PACK - 1, BLOCKS, P], F32, name="turned_sb", tag="stage")
-        for t in range(PACK - 2):
-            terms = look_up(t)
-            turned = psum.tile([P, BLOCKS, P], F32, name="turned", tag="turned%d" % t)
-            for b in range(BLOCKS):
-                for d in range(TERMS):
-                    add_turned(turned[:, b, :], terms, b, d)
-            nc.scalar.copy(turned_sb[:, t, :, :], turned[:])
+        turned = [psum.tile([P, 2, 2, P // 2], F32, name="turned", tag="bank%d" % b) for b in range(BLOCKS)]
+        for half in range(2):
+            terms = look_up(half)
+            for d in range(TERMS):
+                for b in range(BLOCKS):
+                    add_turned(turned[b][:, half, :, :].rearrange("v i m -> v (i m)"), terms, b, d)
+        for b in range(BLOCKS):
+            nc.scalar.copy(
+                turned_sb[:, 0:2, b, :].rearrange("v i (half m) -> v i half m", half=2),
+                turned[b][:].rearrange("v half i m -> v i half m"),
+            )
+        for b in range(BLOCKS):
+            turn_back(b, slice(0, 2), "back%d" % b)
         terms = look_up(PACK - 2)
-        turned_by_block = [psum.tile([P, P], F32, name="turned_block", tag="bank%d" % b) for b in range(BLOCKS)]
+        turned_by_block = [psum.tile([P, P], F32, name="turned_block", tag="turned%d" % b) for b in range(BLOCKS)]
         for d in range(TERMS):
             for b in range(BLOCKS):
                 add_turned(turned_by_block[b][:], terms, b, d)
         for b in range(BLOCKS):
             nc.scalar.copy(turned_sb[:, PACK - 2, b, :], turned_by_block[b][:])
-        turn_back(0)
+        for b in range(BLOCKS):
+            turn_back(b, slice(2, 3), "bank%d" % b)
         nc.vector.quantize_mx(
             out=w2_words[:].bitcast(FP8X4), scales=w2_scales[:], in_=w2_bf[:].rearrange("p t m j -> p (t m j)")
         )
 
-        terms = look_up(PACK - 1)
-        nc.vector.tensor_tensor(terms[0][:], terms[0][:], terms[1][:], ALU.add)
+        last = h[PACK - 1]
+        near = [keep.tile([P, V], F32, name="near%d" % d) for d in range(TERMS)]
+        nc.vector.tensor_tensor(near[0][:], last[:].indirect(pos1_sb[:]), gate_scaled[:, 0, :], ALU.mult)
+        list_cols = [slice(tg.start // LIST_ROWS, tg.stop // LIST_ROWS) for tg in targets]
         for b in range(BLOCKS):
-            nc.vector.tensor_tensor(u[b][:, PACK - 1, :], terms[0][:, targets[b]], terms[2][:, targets[b]], ALU.add)
+            nc.vector.tensor_tensor(
+                near[1][:, targets[b]], last[:].indirect(pos2_sb[:, list_cols[b]]), gate_scaled[:, 1, targets[b]], ALU.mult
+            )
+        for b in range(BLOCKS):
+            nc.vector.tensor_tensor(near[2][:, targets[b]], near[0][:, targets[b]], near[1][:, targets[b]], ALU.add)
+        for b in range(BLOCKS):
+            entries = cen_sb[:, list_cols[b]]
+            nc.vector.tensor_tensor(u[b][:, PACK - 1, :], last[:].indirect(entries), near[2][:, targets[b]], ALU.add)
 
         finish_block(0)
-        turn_back(1)
         finish_block(1)
         for q in range(QUADRANTS):
             queue = nc.sync if q % 2 == 0 else nc.scalar

@@ -32,6 +32,7 @@ NEAR_SCALE = 0.54
 
 H0_PIECES = [slice(0, 256), slice(256, 384), slice(384, 512)]
 SCALAR_SHARE = 48
+Y_BANKS = [["bank2", "bank3", "back0", "back1"], ["turned0", "turned1", "bank0", "bank1"]]
 
 
 def deal(copy, grouped, raw, pair):
@@ -173,19 +174,18 @@ def tile_picked_zgcnii_relu_po_kernel(
             nc.scalar.copy(u[b][:, tiles, :], back[:])
 
         def finish_block(b):
-            z_bf = keep.tile([P, BLOCK, PACK], BF16, name="z_bf%d" % b, align_bytes=64)
+            z_bf = keep.tile([P, BLOCK, PACK], BF16, name="z_bf%d" % b, tag="way%d" % b, align_bytes=64)
             z_words = keep.tile([P, BLOCK], U32, name="z_words%d" % b, align_bytes=64)
             z_scales = keep.tile([P, BLOCK], U8, name="z_scales%d" % b, align_bytes=64)
             nc.scalar.activation(*side_by_side(z_bf[:], u[b][:]), ACT.Copy, scale=Z_SCALE)
             nc.vector.quantize_mx(
                 out=z_words[:].bitcast(FP8X4), scales=z_scales[:], in_=z_bf[:].rearrange("p v t -> p (v t)")
             )
-            y = psum.tile([P, PACK, BLOCK], F32, name="y%d" % b, tag="bank%d" % (b + 2))
-            result = keep.tile([P, PACK, BLOCK], F32, name="result%d" % b)
+            y = [psum.tile([P, BLOCK], F32, name="y%d_%d" % (b, t), tag=Y_BANKS[b][t]) for t in range(PACK)]
             for t in range(PACK):
                 cols = slice(t * P, (t + 1) * P)
                 nc.tensor.matmul_mx(
-                    out=y[:, t, :],
+                    out=y[t][:],
                     lhsT=w2_words[:, cols].bitcast(FP8X4),
                     lhsT_scale=w2_scales[:, cols],
                     rhs=z_words[:].bitcast(FP8X4),
@@ -193,25 +193,26 @@ def tile_picked_zgcnii_relu_po_kernel(
                     start=True,
                     stop=True,
                 )
+            return y
+
+        def way_out(b, y):
+            result = keep.tile([P, PACK, BLOCK], F32, name="result%d" % b, tag="way%d" % (1 - b), align_bytes=64)
             for t in range(PACK):
                 nc.vector.scalar_tensor_tensor(
-                    result[:, t, :], y[:, t, :], turn_scaled[:, t : t + 1], u[b][:, t, :], ALU.mult, ALU.add
+                    result[:, t, :], y[t][:], turn_scaled[:, t : t + 1], u[b][:, t, :], ALU.mult, ALU.add
                 )
-            nc.sync.dma_start(out_0_rows[:, :, targets[b]], result[:])
-
-            result_bf = keep.tile([P, BLOCK, PACK], BF16, name="result_bf%d" % b, align_bytes=64)
+                if b == BLOCKS - 1 and t % 2 == 1:
+                    nc.sync.dma_start(out_0_rows[:, t - 1 : t + 1, targets[b]], result[:, t - 1 : t + 1, :])
             if b < BLOCKS - 1:
-                nc.scalar.activation(*side_by_side(result_bf[:], result[:]), ACT.Copy, scale=1.0)
+                nc.sync.dma_start(out_0_rows[:, :, targets[b]], result[:])
+
+            result_bf = result_bf_all[:, targets[b], :]
+            if b < BLOCKS - 1:
+                nc.scalar.activation(*side_by_side(result_bf, result[:]), ACT.Copy, scale=1.0)
             else:
                 first, rest = slice(0, SCALAR_SHARE), slice(SCALAR_SHARE, BLOCK)
                 nc.scalar.activation(*side_by_side(result_bf[:, first, :], result[:, :, first]), ACT.Copy, scale=1.0)
                 nc.vector.tensor_copy(*side_by_side(result_bf[:, rest, :], result[:, :, rest]))
-            nc.vector.quantize_mx(
-                out=out_words[:, targets[b]].bitcast(FP8X4),
-                scales=out_scales[:, targets[b]],
-                in_=result_bf[:].rearrange("p v t -> p (v t)"),
-            )
-            nc.sync.dma_start(out_1_words[:, targets[b]], out_words[:, targets[b]].bitcast(I32))
 
         nc.scalar.activation(gate_scaled[:], gate_raw[:], ACT.Copy, scale=GATE_SCALE)
         nc.scalar.activation(turn_scaled[:], turn_raw[:], ACT.Copy, scale=TURN_SCALE)
@@ -259,8 +260,17 @@ def tile_picked_zgcnii_relu_po_kernel(
             entries = cen_sb[:, list_cols[b]]
             nc.vector.tensor_tensor(u[b][:, PACK - 1, :], last[:].indirect(entries), near[2][:, targets[b]], ALU.add)
 
-        finish_block(0)
-        finish_block(1)
+        products = [finish_block(b) for b in range(BLOCKS)]
+        result_bf_all = keep.tile([P, V, PACK], BF16, name="result_bf", align_bytes=64)
+        for b in range(BLOCKS):
+            way_out(b, products[b])
+        for b in range(BLOCKS):
+            nc.vector.quantize_mx(
+                out=out_words[:, targets[b]].bitcast(FP8X4),
+                scales=out_scales[:, targets[b]],
+                in_=result_bf_all[:, targets[b], :].rearrange("p v t -> p (v t)"),
+            )
+        nc.sync.dma_start(out_1_words, out_words[:].bitcast(I32))
         for q in range(QUADRANTS):
             queue = nc.sync if q % 2 == 0 else nc.scalar
             queue.dma_start(

@@ -43,7 +43,7 @@ def deal(copy, grouped, raw, pair):
 
 
 def side_by_side(packed, row_tiles):
-    return packed.rearrange("p (c i) t -> p c t i", i=2), row_tiles.rearrange("p t (c i) -> p c t i", i=2)
+    return packed.rearrange("p (c i) t -> p c t i", i=4), row_tiles.rearrange("p t (c i) -> p c t i", i=4)
 
 
 def tile_picked_zgcnii_relu_po_kernel(
@@ -100,7 +100,7 @@ def tile_picked_zgcnii_relu_po_kernel(
         nc.vector.tensor_copy(picked_scales[:], x_scale_table[:].indirect(offs_sb[:]))
 
         w1_half_bf = [keep.tile([P, 2, P // 2, PACK], BF16, name="w1_half_bf%d" % i, tag=tag, align_bytes=64) for i, tag in enumerate(["w1_first_bf", "term0_0"])]
-        w1_rest_bf = keep.tile([P, 2, P, PACK], BF16, name="w1_rest_bf", tag="term2_0", align_bytes=64)
+        w1_rest_bf = [keep.tile([P, 2, P // 2, PACK], BF16, name="w1_rest_bf%d" % i, tag=tag, align_bytes=64) for i, tag in enumerate(["w1_low_bf", "term2_0"])]
         w1_words = keep.tile([P, H], U32, name="w1_words", tag="weights", align_bytes=64)
         w1_scales = keep.tile([P, H], U8, name="w1_scales", align_bytes=64)
         gate_scaled = keep.tile([P, 2, V], F32, name="gate_scaled")
@@ -109,7 +109,7 @@ def tile_picked_zgcnii_relu_po_kernel(
             nc.vector.quantize_mx(
                 out=w1_words[:, cols].bitcast(FP8X4),
                 scales=w1_scales[:, cols],
-                in_=grouped[:].rearrange("p i m j -> p (i m j)"),
+                in_=grouped.rearrange("p i m j -> p (i m j)"),
             )
 
         def first_product(t, entries, bank):
@@ -128,20 +128,22 @@ def tile_picked_zgcnii_relu_po_kernel(
 
         h = [keep.tile([P, S], F32, name="h%d" % t) for t in range(PACK)]
         deal(nc.vector.tensor_copy, w1_half_bf[0][:], w1_raw[0], 0)
-        deal(nc.scalar.copy, w1_rest_bf[:, :, 0 : P // 2, :], w1_raw[0], 1)
-        quantize_w1(slice(0, P), w1_half_bf[0])
+        deal(nc.scalar.copy, w1_rest_bf[0][:], w1_raw[0], 1)
+        quantize_w1(slice(0, P), w1_half_bf[0][:])
+        quantize_w1(slice(2 * P, 2 * P + P // 2), w1_rest_bf[0][:, 0:1])
+        quantize_w1(slice(H - P // 2, H), w1_rest_bf[0][:, 1:2])
         for i, piece in enumerate(H0_PIECES):
             entries = offs_sb[:, piece.start // LIST_ROWS : piece.stop // LIST_ROWS]
             nc.vector.tensor_copy(picked_words[:, piece], x_word_table[:].indirect(entries))
             acc = first_product(0, piece, i)
             nc.scalar.activation(h[0][:, piece], acc[:], ACT.Relu, scale=NEAR_SCALE)
         deal(nc.vector.tensor_copy, w1_half_bf[1][:], w1_raw[1], 0)
-        deal(nc.scalar.copy, w1_rest_bf[:, :, P // 2 : P, :], w1_raw[1], 1)
-        quantize_w1(slice(P, 2 * P), w1_half_bf[1])
+        deal(nc.scalar.copy, w1_rest_bf[1][:], w1_raw[1], 1)
+        quantize_w1(slice(P, 2 * P), w1_half_bf[1][:])
         for t in range(1, PACK):
             if t == 2:
-                quantize_w1(slice(2 * P, H), w1_rest_bf)
-            acc = first_product(t, slice(0, S), (t + 2) % 4)
+                quantize_w1(slice(2 * P + P // 2, H - P // 2), w1_rest_bf[1][:])
+            acc = first_product([0, 1, 3, 2][t], slice(0, S), (t + 2) % 4)
             nc.scalar.activation(h[t][:], acc[:], ACT.Relu, scale=H_SCALE if t == PACK - 1 else NEAR_SCALE)
 
         w2_bf = keep.tile([P, PACK, P, PACK], BF16, name="w2_bf", tag="weights", align_bytes=64)
@@ -171,7 +173,8 @@ def tile_picked_zgcnii_relu_po_kernel(
             back = psum.tile([P, tiles.stop - tiles.start, BLOCK], F32, name="back", tag=tag)
             for t in range(tiles.start, tiles.stop):
                 nc.tensor.transpose(back[:, t - tiles.start, :], turned_sb[:, t, b, :], ident[:])
-            nc.scalar.copy(u[b][:, tiles, :], back[:])
+            rows = tiles if tiles.start == 0 else slice(3, 4)
+            nc.scalar.copy(u[b][:, rows, :], back[:])
 
         def finish_block(b):
             z_bf = keep.tile([P, BLOCK, PACK], BF16, name="z_bf%d" % b, tag="way%d" % b, align_bytes=64)
@@ -239,7 +242,10 @@ def tile_picked_zgcnii_relu_po_kernel(
             for b in range(BLOCKS):
                 add_turned(turned_by_block[b][:], terms, b, d)
         for b in range(BLOCKS):
-            nc.scalar.copy(turned_sb[:, PACK - 2, b, :], turned_by_block[b][:])
+            nc.scalar.copy(
+                turned_sb[:, PACK - 2, b, :].rearrange("v (half m) -> v half m", half=2),
+                turned_by_block[b][:].rearrange("v (half m) -> v half m", half=2)[:, ::-1, :],
+            )
         for b in range(BLOCKS):
             turn_back(b, slice(2, 3), "bank%d" % b)
         nc.vector.quantize_mx(
@@ -258,7 +264,7 @@ def tile_picked_zgcnii_relu_po_kernel(
             nc.vector.tensor_tensor(near[2][:, targets[b]], near[0][:, targets[b]], near[1][:, targets[b]], ALU.add)
         for b in range(BLOCKS):
             entries = cen_sb[:, list_cols[b]]
-            nc.vector.tensor_tensor(u[b][:, PACK - 1, :], last[:].indirect(entries), near[2][:, targets[b]], ALU.add)
+            nc.vector.tensor_tensor(u[b][:, 2, :], last[:].indirect(entries), near[2][:, targets[b]], ALU.add)
 
         products = [finish_block(b) for b in range(BLOCKS)]
         result_bf_all = keep.tile([P, V, PACK], BF16, name="result_bf", align_bytes=64)

@@ -204,10 +204,8 @@ def tile_picked_zgcnii_relu_po_kernel(
                 nc.vector.scalar_tensor_tensor(
                     result[:, t, :], y[t][:], turn_scaled[:, t : t + 1], u[b][:, t, :], ALU.mult, ALU.add
                 )
-                if b == BLOCKS - 1 and t % 2 == 1:
+                if t % 2 == 1:
                     nc.sync.dma_start(out_0_rows[:, t - 1 : t + 1, targets[b]], result[:, t - 1 : t + 1, :])
-            if b < BLOCKS - 1:
-                nc.sync.dma_start(out_0_rows[:, :, targets[b]], result[:])
 
             result_bf = result_bf_all[:, targets[b], :]
             if b < BLOCKS - 1:

@@ -199,17 +199,19 @@ def tile_picked_zgcnii_relu_po_kernel(
             return y
 
         def way_out(b, y):
-            result = keep.tile([P, PACK, BLOCK], F32, name="result%d" % b, tag="way%d" % (1 - b), align_bytes=64)
+            result = result_all[:, :, targets[b]]
             for t in range(PACK):
                 nc.vector.scalar_tensor_tensor(
                     result[:, t, :], y[t][:], turn_scaled[:, t : t + 1], u[b][:, t, :], ALU.mult, ALU.add
                 )
-                if t % 2 == 1:
-                    nc.sync.dma_start(out_0_rows[:, t - 1 : t + 1, targets[b]], result[:, t - 1 : t + 1, :])
+                if t == 1:
+                    nc.sync.dma_start(out_0_rows[:, 0:2, targets[b]], result[:, 0:2, :])
+            if b == BLOCKS - 1:
+                nc.sync.dma_start(out_0_rows[:, 2:PACK, :], result_all[:, 2:PACK, :])
 
             result_bf = result_bf_all[:, targets[b], :]
             if b < BLOCKS - 1:
-                nc.scalar.activation(*side_by_side(result_bf, result[:]), ACT.Copy, scale=1.0)
+                nc.scalar.activation(*side_by_side(result_bf, result), ACT.Copy, scale=1.0)
             else:
                 first, rest = slice(0, SCALAR_SHARE), slice(SCALAR_SHARE, BLOCK)
                 nc.scalar.activation(*side_by_side(result_bf[:, first, :], result[:, :, first]), ACT.Copy, scale=1.0)
@@ -265,6 +267,7 @@ def tile_picked_zgcnii_relu_po_kernel(
             nc.vector.tensor_tensor(u[b][:, 2, :], last[:].indirect(entries), near[2][:, targets[b]], ALU.add)
 
         products = [finish_block(b) for b in range(BLOCKS)]
+        result_all = keep.tile([P, PACK, V], F32, name="result_all", tag="way1", align_bytes=64)
         result_bf_all = keep.tile([P, V, PACK], BF16, name="result_bf", align_bytes=64)
         for b in range(BLOCKS):
             way_out(b, products[b])

@@ -42,6 +42,13 @@ def deal(copy, grouped, raw, pair):
     )
 
 
+def deal_quarter(copy, grouped, raw, quarter):
+    copy(
+        out=grouped[quarter][:].rearrange("p i m j -> p m j i"),
+        in_=raw[:, :, quarter * P : (quarter + 1) * P].rearrange("p j (m t) -> p m j t", t=PACK)[:, :, :, 0:2],
+    )
+
+
 def side_by_side(packed, row_tiles):
     return packed.rearrange("p (c i) t -> p c t i", i=4), row_tiles.rearrange("p t (c i) -> p c t i", i=4)
 
@@ -60,7 +67,7 @@ def tile_picked_zgcnii_relu_po_kernel(
         pos2_sb = keep.tile([P, V // LIST_ROWS], U16, name="pos2_sb")
         x_word_table = keep.tile([P, T], U32, name="x_word_table")
         x_scale_table = keep.tile([P, T], U8, name="x_scale_table")
-        w1_raw = [keep.tile([P, PACK, H // 2], F32, name="w1_raw%d" % half) for half in range(2)]
+        w1_raw = [keep.tile([P, PACK, H // 2], F32, name="w1_raw%d" % half, tag=tag, align_bytes=64) for half, tag in enumerate(["w1_raw0", "term2_0"])]
         w2_raw = keep.tile([P, PACK, H], F32, name="w2_raw", tag="stage")
         turn_raw = keep.tile([P, PACK], F32, name="turn_raw")
         x_scale_rows = keep.tile([P, T], U8, name="x_scale_rows")
@@ -95,12 +102,17 @@ def tile_picked_zgcnii_relu_po_kernel(
         ones = keep.tile([P, V], F32, name="ones")
         nc.vector.memset(ones[:], 1.0)
         nc.vector.tensor_scalar_mul(centre_share[:], ones[:], 1.0 / GATE_SCALE)
+        z_scale = keep.tile([P, 1], F32, name="z_scale", tag="results", align_bytes=64)
+        nc.vector.tensor_scalar_mul(z_scale[:], ones[:, 0:1], Z_SCALE)
         picked_words = keep.tile([P, S], U32, name="picked_words", align_bytes=64)
         picked_scales = keep.tile([P, S], U8, name="picked_scales", align_bytes=64)
         nc.vector.tensor_copy(picked_scales[:], x_scale_table[:].indirect(offs_sb[:]))
 
-        w1_half_bf = [keep.tile([P, 2, P // 2, PACK], BF16, name="w1_half_bf%d" % i, tag=tag, align_bytes=64) for i, tag in enumerate(["w1_first_bf", "term0_0"])]
-        w1_rest_bf = [keep.tile([P, 2, P // 2, PACK], BF16, name="w1_rest_bf%d" % i, tag=tag, align_bytes=64) for i, tag in enumerate(["w1_low_bf", "term2_0"])]
+        w1_half_bf = [
+            [keep.tile([P, 2, P // 4, PACK], BF16, name="w1_bf%d_%d" % (i, quarter), tag=tag, align_bytes=64) for quarter, tag in enumerate(tags)]
+            for i, tags in enumerate([["w1_bf0_0", "w1_bf0_1"], ["term0_0", "w1_bf1_1"]])
+        ]
+        w1_rest_bf = [keep.tile([P, 2, P // 2, PACK], BF16, name="w1_rest_bf%d" % i, tag=tag, align_bytes=64) for i, tag in enumerate(["w1_low_bf", "w1_high_bf"])]
         w1_words = keep.tile([P, H], U32, name="w1_words", tag="weights", align_bytes=64)
         w1_scales = keep.tile([P, H], U8, name="w1_scales", align_bytes=64)
         gate_scaled = keep.tile([P, 2, V], F32, name="gate_scaled")
@@ -127,9 +139,11 @@ def tile_picked_zgcnii_relu_po_kernel(
             return acc
 
         h = [keep.tile([P, S], F32, name="h%d" % t) for t in range(PACK)]
-        deal(nc.vector.tensor_copy, w1_half_bf[0][:], w1_raw[0], 0)
+        for quarter in range(2):
+            deal_quarter(nc.vector.tensor_copy, w1_half_bf[0], w1_raw[0], quarter)
         deal(nc.scalar.copy, w1_rest_bf[0][:], w1_raw[0], 1)
-        quantize_w1(slice(0, P), w1_half_bf[0][:])
+        for quarter in range(2):
+            quantize_w1(slice(quarter * P // 2, (quarter + 1) * P // 2), w1_half_bf[0][quarter][:])
         quantize_w1(slice(2 * P, 2 * P + P // 2), w1_rest_bf[0][:, 0:1])
         quantize_w1(slice(H - P // 2, H), w1_rest_bf[0][:, 1:2])
         for i, piece in enumerate(H0_PIECES):
@@ -137,9 +151,11 @@ def tile_picked_zgcnii_relu_po_kernel(
             nc.vector.tensor_copy(picked_words[:, piece], x_word_table[:].indirect(entries))
             acc = first_product(0, piece, i)
             nc.scalar.activation(h[0][:, piece], acc[:], ACT.Relu, scale=NEAR_SCALE)
-        deal(nc.vector.tensor_copy, w1_half_bf[1][:], w1_raw[1], 0)
+        for quarter in range(2):
+            deal_quarter(nc.vector.tensor_copy, w1_half_bf[1], w1_raw[1], quarter)
         deal(nc.scalar.copy, w1_rest_bf[1][:], w1_raw[1], 1)
-        quantize_w1(slice(P, 2 * P), w1_half_bf[1][:])
+        for quarter in range(2):
+            quantize_w1(slice(P + quarter * P // 2, P + (quarter + 1) * P // 2), w1_half_bf[1][quarter][:])
         for t in range(1, PACK):
             if t == 2:
                 quantize_w1(slice(2 * P + P // 2, H - P // 2), w1_rest_bf[1][:])
@@ -180,7 +196,7 @@ def tile_picked_zgcnii_relu_po_kernel(
             z_bf = keep.tile([P, BLOCK, PACK], BF16, name="z_bf%d" % b, tag="way%d" % b, align_bytes=64)
             z_words = keep.tile([P, BLOCK], U32, name="z_words%d" % b, align_bytes=64)
             z_scales = keep.tile([P, BLOCK], U8, name="z_scales%d" % b, align_bytes=64)
-            nc.scalar.activation(*side_by_side(z_bf[:], u[b][:]), ACT.Copy, scale=Z_SCALE)
+            nc.scalar.activation(*side_by_side(z_bf[:], u[b][:]), ACT.Copy, scale=z_scale[:])
             nc.vector.quantize_mx(
                 out=z_words[:].bitcast(FP8X4), scales=z_scales[:], in_=z_bf[:].rearrange("p v t -> p (v t)")
             )
@@ -223,16 +239,16 @@ def tile_picked_zgcnii_relu_po_kernel(
             deal(nc.scalar.copy, w2_bf[:, 2 * pair : 2 * pair + 2, :, :], w2_raw, pair)
 
         turned_sb = keep.tile([P, PACK - 1, BLOCKS, P], F32, name="turned_sb", tag="stage")
-        turned = [psum.tile([P, 2, 2, P // 2], F32, name="turned", tag="bank%d" % b) for b in range(BLOCKS)]
+        turned = [psum.tile([P, 2, P], F32, name="turned", tag="bank%d" % b) for b in range(BLOCKS)]
         for half in range(2):
             terms = look_up(half)
             for d in range(TERMS):
                 for b in range(BLOCKS):
-                    add_turned(turned[b][:, half, :, :].rearrange("v i m -> v (i m)"), terms, b, d)
+                    add_turned(turned[b][:, half, :], terms, b, d)
         for b in range(BLOCKS):
             nc.scalar.copy(
-                turned_sb[:, 0:2, b, :].rearrange("v i (half m) -> v i half m", half=2),
-                turned[b][:].rearrange("v half i m -> v i half m"),
+                turned_sb[:, 0:2, b, :].rearrange("v i (quarter m) -> v i quarter m", quarter=4),
+                turned[b][:].rearrange("v half (low i m) -> v i (half low) m", low=2, i=2),
             )
         for b in range(BLOCKS):
             turn_back(b, slice(0, 2), "back%d" % b)
@@ -267,7 +283,7 @@ def tile_picked_zgcnii_relu_po_kernel(
             nc.vector.tensor_tensor(u[b][:, 2, :], last[:].indirect(entries), near[2][:, targets[b]], ALU.add)
 
         products = [finish_block(b) for b in range(BLOCKS)]
-        result_all = keep.tile([P, PACK, V], F32, name="result_all", tag="way1", align_bytes=64)
+        result_all = keep.tile([P, PACK, V], F32, name="result_all", tag="results", align_bytes=64)
         result_bf_all = keep.tile([P, V, PACK], BF16, name="result_bf", align_bytes=64)
         for b in range(BLOCKS):
             way_out(b, products[b])

@@ -31,7 +31,8 @@ TURN_SCALE = 0.4
 NEAR_SCALE = 0.54
 
 H0_PIECES = [slice(0, 256), slice(256, 384), slice(384, 512)]
-SCALAR_SHARE = 48
+SCALAR_SHARE = [96, 32]
+Z_SCALAR_SHARE = 80
 Y_BANKS = [["bank2", "bank3", "back0", "back1"], ["turned0", "turned1", "bank0", "bank1"]]
 
 
@@ -102,8 +103,9 @@ def tile_picked_zgcnii_relu_po_kernel(
         ones = keep.tile([P, V], F32, name="ones")
         nc.vector.memset(ones[:], 1.0)
         nc.vector.tensor_scalar_mul(centre_share[:], ones[:], 1.0 / GATE_SCALE)
-        z_scale = keep.tile([P, 1], F32, name="z_scale", tag="results", align_bytes=64)
-        nc.vector.tensor_scalar_mul(z_scale[:], ones[:, 0:1], Z_SCALE)
+        z_scale = [keep.tile([P, 1], F32, name="z_scale%d" % b, tag=tag, align_bytes=64) for b, tag in enumerate(["w2_high", "results"])]
+        for b in range(BLOCKS):
+            nc.vector.tensor_scalar_mul(z_scale[b][:], ones[:, 0:1], Z_SCALE)
         picked_words = keep.tile([P, S], U32, name="picked_words", align_bytes=64)
         picked_scales = keep.tile([P, S], U8, name="picked_scales", align_bytes=64)
         nc.vector.tensor_copy(picked_scales[:], x_scale_table[:].indirect(offs_sb[:]))
@@ -163,8 +165,16 @@ def tile_picked_zgcnii_relu_po_kernel(
             nc.scalar.activation(h[t][:], acc[:], ACT.Relu, scale=H_SCALE if t == PACK - 1 else NEAR_SCALE)
 
         w2_bf = keep.tile([P, PACK, P, PACK], BF16, name="w2_bf", tag="weights", align_bytes=64)
-        w2_words = keep.tile([P, H], U32, name="w2_words", align_bytes=64)
+        w2_words = [keep.tile([P, H // 2], U32, name="w2_words%d" % i, tag=tag, align_bytes=64) for i, tag in enumerate(["w2_low", "w2_high"])]
         w2_scales = keep.tile([P, H], U8, name="w2_scales", align_bytes=64)
+
+        def quantize_w2(pair):
+            nc.vector.quantize_mx(
+                out=w2_words[pair][:].bitcast(FP8X4),
+                scales=w2_scales[:, pair * 2 * P : (pair + 1) * 2 * P],
+                in_=w2_bf[:, 2 * pair : 2 * pair + 2, :, :].rearrange("p t m j -> p (t m j)"),
+            )
+
         turn_scaled = keep.tile([P, PACK], F32, name="turn_scaled")
         out_words = keep.tile([P, V], U32, name="out_words", align_bytes=64)
         out_scales = keep.tile([P, V], U8, name="out_scales", align_bytes=64)
@@ -196,16 +206,22 @@ def tile_picked_zgcnii_relu_po_kernel(
             z_bf = keep.tile([P, BLOCK, PACK], BF16, name="z_bf%d" % b, tag="way%d" % b, align_bytes=64)
             z_words = keep.tile([P, BLOCK], U32, name="z_words%d" % b, align_bytes=64)
             z_scales = keep.tile([P, BLOCK], U8, name="z_scales%d" % b, align_bytes=64)
-            nc.scalar.activation(*side_by_side(z_bf[:], u[b][:]), ACT.Copy, scale=z_scale[:])
+            first, rest = slice(0, Z_SCALAR_SHARE), slice(Z_SCALAR_SHARE, BLOCK)
+            nc.scalar.activation(*side_by_side(z_bf[:, first, :], u[b][:, :, first]), ACT.Copy, scale=z_scale[b][:])
+            nc.vector.tensor_scalar_mul(*side_by_side(z_bf[:, rest, :], u[b][:, :, rest]), Z_SCALE)
+            quantize_w2(b)
             nc.vector.quantize_mx(
                 out=z_words[:].bitcast(FP8X4), scales=z_scales[:], in_=z_bf[:].rearrange("p v t -> p (v t)")
             )
+            return z_words, z_scales
+
+        def second_product(b, z_words, z_scales):
             y = [psum.tile([P, BLOCK], F32, name="y%d_%d" % (b, t), tag=Y_BANKS[b][t]) for t in range(PACK)]
             for t in range(PACK):
                 cols = slice(t * P, (t + 1) * P)
                 nc.tensor.matmul_mx(
                     out=y[t][:],
-                    lhsT=w2_words[:, cols].bitcast(FP8X4),
+                    lhsT=w2_words[t // 2][:, (t % 2) * P : (t % 2 + 1) * P].bitcast(FP8X4),
                     lhsT_scale=w2_scales[:, cols],
                     rhs=z_words[:].bitcast(FP8X4),
                     rhs_scale=z_scales[:],
@@ -225,13 +241,8 @@ def tile_picked_zgcnii_relu_po_kernel(
             if b == BLOCKS - 1:
                 nc.sync.dma_start(out_0_rows[:, 2:PACK, :], result_all[:, 2:PACK, :])
 
-            result_bf = result_bf_all[:, targets[b], :]
-            if b < BLOCKS - 1:
-                nc.scalar.activation(*side_by_side(result_bf, result), ACT.Copy, scale=1.0)
-            else:
-                first, rest = slice(0, SCALAR_SHARE), slice(SCALAR_SHARE, BLOCK)
-                nc.scalar.activation(*side_by_side(result_bf[:, first, :], result[:, :, first]), ACT.Copy, scale=1.0)
-                nc.vector.tensor_copy(*side_by_side(result_bf[:, rest, :], result[:, :, rest]))
+            first = slice(targets[b].start, targets[b].start + SCALAR_SHARE[b])
+            nc.scalar.activation(*side_by_side(result_bf_all[:, first, :], result_all[:, :, first]), ACT.Copy, scale=1.0)
 
         nc.scalar.activation(gate_scaled[:], gate_raw[:], ACT.Copy, scale=GATE_SCALE)
         nc.scalar.activation(turn_scaled[:], turn_raw[:], ACT.Copy, scale=TURN_SCALE)
@@ -264,9 +275,6 @@ def tile_picked_zgcnii_relu_po_kernel(
             )
         for b in range(BLOCKS):
             turn_back(b, slice(2, 3), "bank%d" % b)
-        nc.vector.quantize_mx(
-            out=w2_words[:].bitcast(FP8X4), scales=w2_scales[:], in_=w2_bf[:].rearrange("p t m j -> p (t m j)")
-        )
 
         last = h[PACK - 1]
         near = [keep.tile([P, V], F32, name="near%d" % d) for d in range(TERMS)]
@@ -282,11 +290,15 @@ def tile_picked_zgcnii_relu_po_kernel(
             entries = cen_sb[:, list_cols[b]]
             nc.vector.tensor_tensor(u[b][:, 2, :], last[:].indirect(entries), near[2][:, targets[b]], ALU.add)
 
-        products = [finish_block(b) for b in range(BLOCKS)]
+        z_mx = [finish_block(b) for b in range(BLOCKS)]
+        products = [second_product(b, *z_mx[b]) for b in range(BLOCKS)]
         result_all = keep.tile([P, PACK, V], F32, name="result_all", tag="results", align_bytes=64)
         result_bf_all = keep.tile([P, V, PACK], BF16, name="result_bf", align_bytes=64)
         for b in range(BLOCKS):
             way_out(b, products[b])
+        for b in range(BLOCKS):
+            rest = slice(targets[b].start + SCALAR_SHARE[b], targets[b].stop)
+            nc.vector.tensor_copy(*side_by_side(result_bf_all[:, rest, :], result_all[:, :, rest]))
         for b in range(BLOCKS):
             nc.vector.quantize_mx(
                 out=out_words[:, targets[b]].bitcast(FP8X4),

@@ -21,37 +21,36 @@ PACK = 4
 QUADRANTS = 4
 LIST_ROWS = 16
 TERMS = 3
-BLOCK = 128
-BLOCKS = V // BLOCK
+BATCH = 128
+BATCHES = V // BATCH
+HALF = P // 2
 
-H_SCALE = 0.06
-GATE_SCALE = 9.0
+NEAR_SCALE = 0.54
+CENTRE_SCALE = 0.06
+NEAR_OVER_CENTRE = 9.0
 Z_SCALE = 1.0 / 0.6
 TURN_SCALE = 0.4
-NEAR_SCALE = 0.54
 
 H0_PIECES = [slice(0, 256), slice(256, 384), slice(384, 512)]
-SCALAR_SHARE = [96, 32]
 Z_SCALAR_SHARE = 80
+OUT_SCALAR_SHARE = [64, 56]
+H_TILE_COLUMN = [0, P, 3 * P, 2 * P]
 Y_BANKS = [["bank2", "bank3", "back0", "back1"], ["turned0", "turned1", "bank0", "bank1"]]
 
 
 def deal(copy, grouped, raw, pair):
     copy(
         out=grouped.rearrange("p i m j -> p m j i"),
-        in_=raw[:].rearrange("p j (m t) -> p m j t", t=PACK)[:, :, :, 2 * pair : 2 * pair + 2],
-    )
-
-
-def deal_quarter(copy, grouped, raw, quarter):
-    copy(
-        out=grouped[quarter][:].rearrange("p i m j -> p m j i"),
-        in_=raw[:, :, quarter * P : (quarter + 1) * P].rearrange("p j (m t) -> p m j t", t=PACK)[:, :, :, 0:2],
+        in_=raw.rearrange("p j (m t) -> p m j t", t=PACK)[:, :, :, 2 * pair : 2 * pair + 2],
     )
 
 
 def side_by_side(packed, row_tiles):
     return packed.rearrange("p (c i) t -> p c t i", i=4), row_tiles.rearrange("p t (c i) -> p c t i", i=4)
+
+
+def list_columns(entries):
+    return slice(entries.start // LIST_ROWS, entries.stop // LIST_ROWS)
 
 
 def tile_picked_zgcnii_relu_po_kernel(
@@ -68,7 +67,10 @@ def tile_picked_zgcnii_relu_po_kernel(
         pos2_sb = keep.tile([P, V // LIST_ROWS], U16, name="pos2_sb")
         x_word_table = keep.tile([P, T], U32, name="x_word_table")
         x_scale_table = keep.tile([P, T], U8, name="x_scale_table")
-        w1_raw = [keep.tile([P, PACK, H // 2], F32, name="w1_raw%d" % half, tag=tag, align_bytes=64) for half, tag in enumerate(["w1_raw0", "term2_0"])]
+        w1_raw = [
+            keep.tile([P, PACK, H // 2], F32, name="w1_raw%d" % half, tag=tag, align_bytes=64)
+            for half, tag in enumerate(["w1_raw0", "term2_0"])
+        ]
         w2_raw = keep.tile([P, PACK, H], F32, name="w2_raw", tag="stage")
         turn_raw = keep.tile([P, PACK], F32, name="turn_raw")
         x_scale_rows = keep.tile([P, T], U8, name="x_scale_rows")
@@ -102,33 +104,52 @@ def tile_picked_zgcnii_relu_po_kernel(
         centre_share = keep.tile([P, V], F32, name="centre_share")
         ones = keep.tile([P, V], F32, name="ones")
         nc.vector.memset(ones[:], 1.0)
-        nc.vector.tensor_scalar_mul(centre_share[:], ones[:], 1.0 / GATE_SCALE)
-        z_scale = [keep.tile([P, 1], F32, name="z_scale%d" % b, tag=tag, align_bytes=64) for b, tag in enumerate(["w2_high", "results"])]
-        for b in range(BLOCKS):
-            nc.vector.tensor_scalar_mul(z_scale[b][:], ones[:, 0:1], Z_SCALE)
+        nc.vector.tensor_scalar_mul(centre_share[:], ones[:], 1.0 / NEAR_OVER_CENTRE)
+        z_factor = [
+            keep.tile([P, 1], F32, name="z_factor%d" % b, tag=tag, align_bytes=64)
+            for b, tag in enumerate(["w2_high", "results"])
+        ]
+        for b in range(BATCHES):
+            nc.vector.tensor_scalar_mul(z_factor[b][:], ones[:, 0:1], Z_SCALE)
         picked_words = keep.tile([P, S], U32, name="picked_words", align_bytes=64)
         picked_scales = keep.tile([P, S], U8, name="picked_scales", align_bytes=64)
         nc.vector.tensor_copy(picked_scales[:], x_scale_table[:].indirect(offs_sb[:]))
 
-        w1_half_bf = [
-            [keep.tile([P, 2, P // 4, PACK], BF16, name="w1_bf%d_%d" % (i, quarter), tag=tag, align_bytes=64) for quarter, tag in enumerate(tags)]
-            for i, tags in enumerate([["w1_bf0_0", "w1_bf0_1"], ["term0_0", "w1_bf1_1"]])
+        w1_first_bf = [
+            [
+                keep.tile([P, 2, P // PACK, PACK], BF16, name="w1_bf%d_%d" % (half, part), tag=tag, align_bytes=64)
+                for part, tag in enumerate(tags)
+            ]
+            for half, tags in enumerate([["w1_bf0_0", "w1_bf0_1"], ["term0_0", "w1_bf1_1"]])
         ]
-        w1_rest_bf = [keep.tile([P, 2, P // 2, PACK], BF16, name="w1_rest_bf%d" % i, tag=tag, align_bytes=64) for i, tag in enumerate(["w1_low_bf", "w1_high_bf"])]
+        w1_rest_bf = [
+            keep.tile([P, 2, HALF, PACK], BF16, name="w1_rest_bf%d" % half, align_bytes=64) for half in range(2)
+        ]
         w1_words = keep.tile([P, H], U32, name="w1_words", tag="weights", align_bytes=64)
         w1_scales = keep.tile([P, H], U8, name="w1_scales", align_bytes=64)
-        gate_scaled = keep.tile([P, 2, V], F32, name="gate_scaled")
+        gate1_scaled = keep.tile([P, V], F32, name="gate1_scaled")
 
-        def quantize_w1(cols, grouped):
+        def round_first(half):
+            for part in range(2):
+                deal(nc.vector.tensor_copy, w1_first_bf[half][part][:], w1_raw[half][:, :, part * P : (part + 1) * P], 0)
+
+        def quantize_w1(first_column, grouped):
+            cols = slice(first_column, first_column + grouped.shape[1] * grouped.shape[2])
             nc.vector.quantize_mx(
                 out=w1_words[:, cols].bitcast(FP8X4),
                 scales=w1_scales[:, cols],
                 in_=grouped.rearrange("p i m j -> p (i m j)"),
             )
 
-        def first_product(t, entries, bank):
-            cols = slice(t * P, (t + 1) * P)
-            acc = psum.tile([P, entries.stop - entries.start], F32, name="h_acc", tag="bank%d" % bank)
+        def quantize_first(half):
+            for part in range(2):
+                quantize_w1(H_TILE_COLUMN[half] + part * HALF, w1_first_bf[half][part][:])
+
+        h = [keep.tile([P, S], F32, name="h%d" % t) for t in range(PACK)]
+
+        def first_product(t, entries, bank, factor):
+            cols = slice(H_TILE_COLUMN[t], H_TILE_COLUMN[t] + P)
+            acc = psum.tile([P, entries.stop - entries.start], F32, name="h_acc", tag=bank)
             nc.tensor.matmul_mx(
                 out=acc[:],
                 lhsT=w1_words[:, cols].bitcast(FP8X4),
@@ -138,50 +159,37 @@ def tile_picked_zgcnii_relu_po_kernel(
                 start=True,
                 stop=True,
             )
-            return acc
+            nc.scalar.activation(h[t][:, entries], acc[:], ACT.Relu, scale=factor)
 
-        h = [keep.tile([P, S], F32, name="h%d" % t) for t in range(PACK)]
-        for quarter in range(2):
-            deal_quarter(nc.vector.tensor_copy, w1_half_bf[0], w1_raw[0], quarter)
-        deal(nc.scalar.copy, w1_rest_bf[0][:], w1_raw[0], 1)
-        for quarter in range(2):
-            quantize_w1(slice(quarter * P // 2, (quarter + 1) * P // 2), w1_half_bf[0][quarter][:])
-        quantize_w1(slice(2 * P, 2 * P + P // 2), w1_rest_bf[0][:, 0:1])
-        quantize_w1(slice(H - P // 2, H), w1_rest_bf[0][:, 1:2])
+        round_first(0)
+        deal(nc.scalar.copy, w1_rest_bf[0][:], w1_raw[0][:], 1)
+        quantize_first(0)
+        quantize_w1(2 * P, w1_rest_bf[0][:, 0:1])
+        quantize_w1(H - HALF, w1_rest_bf[0][:, 1:2])
         for i, piece in enumerate(H0_PIECES):
-            entries = offs_sb[:, piece.start // LIST_ROWS : piece.stop // LIST_ROWS]
-            nc.vector.tensor_copy(picked_words[:, piece], x_word_table[:].indirect(entries))
-            acc = first_product(0, piece, i)
-            nc.scalar.activation(h[0][:, piece], acc[:], ACT.Relu, scale=NEAR_SCALE)
-        for quarter in range(2):
-            deal_quarter(nc.vector.tensor_copy, w1_half_bf[1], w1_raw[1], quarter)
-        deal(nc.scalar.copy, w1_rest_bf[1][:], w1_raw[1], 1)
-        for quarter in range(2):
-            quantize_w1(slice(P + quarter * P // 2, P + (quarter + 1) * P // 2), w1_half_bf[1][quarter][:])
-        for t in range(1, PACK):
-            if t == 2:
-                quantize_w1(slice(2 * P + P // 2, H - P // 2), w1_rest_bf[1][:])
-            acc = first_product([0, 1, 3, 2][t], slice(0, S), (t + 2) % 4)
-            nc.scalar.activation(h[t][:], acc[:], ACT.Relu, scale=H_SCALE if t == PACK - 1 else NEAR_SCALE)
+            nc.vector.tensor_copy(picked_words[:, piece], x_word_table[:].indirect(offs_sb[:, list_columns(piece)]))
+            first_product(0, piece, "bank%d" % i, NEAR_SCALE)
+        round_first(1)
+        deal(nc.scalar.copy, w1_rest_bf[1][:], w1_raw[1][:], 1)
+        quantize_first(1)
+        first_product(1, slice(0, S), "bank3", NEAR_SCALE)
+        quantize_w1(2 * P + HALF, w1_rest_bf[1][:])
+        first_product(2, slice(0, S), "bank0", NEAR_SCALE)
+        first_product(3, slice(0, S), "bank1", CENTRE_SCALE)
 
         w2_bf = keep.tile([P, PACK, P, PACK], BF16, name="w2_bf", tag="weights", align_bytes=64)
-        w2_words = [keep.tile([P, H // 2], U32, name="w2_words%d" % i, tag=tag, align_bytes=64) for i, tag in enumerate(["w2_low", "w2_high"])]
+        w2_words = [
+            keep.tile([P, H // 2], U32, name="w2_words%d" % pair, tag=tag, align_bytes=64)
+            for pair, tag in enumerate(["w2_low", "w2_high"])
+        ]
         w2_scales = keep.tile([P, H], U8, name="w2_scales", align_bytes=64)
-
-        def quantize_w2(pair):
-            nc.vector.quantize_mx(
-                out=w2_words[pair][:].bitcast(FP8X4),
-                scales=w2_scales[:, pair * 2 * P : (pair + 1) * 2 * P],
-                in_=w2_bf[:, 2 * pair : 2 * pair + 2, :, :].rearrange("p t m j -> p (t m j)"),
-            )
-
         turn_scaled = keep.tile([P, PACK], F32, name="turn_scaled")
         out_words = keep.tile([P, V], U32, name="out_words", align_bytes=64)
         out_scales = keep.tile([P, V], U8, name="out_scales", align_bytes=64)
         out_0_rows = out_0.rearrange("(p t) v -> p t v", t=PACK)
         out_1_words = out_1[0].rearrange("p c r -> p (c r)").bitcast(I32)
-        u = [keep.tile([P, PACK, BLOCK], F32, name="u%d" % b) for b in range(BLOCKS)]
-        targets = [slice(b * BLOCK, (b + 1) * BLOCK) for b in range(BLOCKS)]
+        u = [keep.tile([P, PACK, BATCH], F32, name="u%d" % b) for b in range(BATCHES)]
+        targets = [slice(b * BATCH, (b + 1) * BATCH) for b in range(BATCHES)]
 
         def look_up(t):
             terms = [keep.tile([P, V], F32, name="term%d_%d" % (d, t), align_bytes=64) for d in range(TERMS)]
@@ -190,39 +198,48 @@ def tile_picked_zgcnii_relu_po_kernel(
             nc.vector.tensor_tensor(terms[2][:], h[t][:].indirect(pos2_sb[:]), gate_raw[:, 1, :], ALU.mult)
             return terms
 
-        def add_turned(total, terms, b, d):
-            nc.tensor.matmul(
-                total, terms[d][:, targets[b]], ident[:], start=(d == 0), stop=(d == TERMS - 1), is_transpose=True
-            )
+        def add_turned(totals, terms):
+            for d in range(TERMS):
+                for b in range(BATCHES):
+                    nc.tensor.matmul(
+                        totals[b],
+                        terms[d][:, targets[b]],
+                        ident[:],
+                        start=(d == 0),
+                        stop=(d == TERMS - 1),
+                        is_transpose=True,
+                    )
 
-        def turn_back(b, tiles, tag):
-            back = psum.tile([P, tiles.stop - tiles.start, BLOCK], F32, name="back", tag=tag)
-            for t in range(tiles.start, tiles.stop):
-                nc.tensor.transpose(back[:, t - tiles.start, :], turned_sb[:, t, b, :], ident[:])
-            rows = tiles if tiles.start == 0 else slice(3, 4)
+        def turn_back(b, places, rows, bank):
+            back = psum.tile([P, places.stop - places.start, BATCH], F32, name="back", tag=bank)
+            for place in range(places.start, places.stop):
+                nc.tensor.transpose(back[:, place - places.start, :], turned_sb[:, place, b, :], ident[:])
             nc.scalar.copy(u[b][:, rows, :], back[:])
 
-        def finish_block(b):
-            z_bf = keep.tile([P, BLOCK, PACK], BF16, name="z_bf%d" % b, tag="way%d" % b, align_bytes=64)
-            z_words = keep.tile([P, BLOCK], U32, name="z_words%d" % b, align_bytes=64)
-            z_scales = keep.tile([P, BLOCK], U8, name="z_scales%d" % b, align_bytes=64)
-            first, rest = slice(0, Z_SCALAR_SHARE), slice(Z_SCALAR_SHARE, BLOCK)
-            nc.scalar.activation(*side_by_side(z_bf[:, first, :], u[b][:, :, first]), ACT.Copy, scale=z_scale[b][:])
+        def quantize_z(b):
+            z_bf = keep.tile([P, BATCH, PACK], BF16, name="z_bf%d" % b, align_bytes=64)
+            z_words = keep.tile([P, BATCH], U32, name="z_words%d" % b, align_bytes=64)
+            z_scales = keep.tile([P, BATCH], U8, name="z_scales%d" % b, align_bytes=64)
+            first, rest = slice(0, Z_SCALAR_SHARE), slice(Z_SCALAR_SHARE, BATCH)
+            nc.scalar.activation(*side_by_side(z_bf[:, first, :], u[b][:, :, first]), ACT.Copy, scale=z_factor[b][:])
             nc.vector.tensor_scalar_mul(*side_by_side(z_bf[:, rest, :], u[b][:, :, rest]), Z_SCALE)
-            quantize_w2(b)
+            nc.vector.quantize_mx(
+                out=w2_words[b][:].bitcast(FP8X4),
+                scales=w2_scales[:, 2 * b * P : 2 * (b + 1) * P],
+                in_=w2_bf[:, 2 * b : 2 * b + 2, :, :].rearrange("p t m j -> p (t m j)"),
+            )
             nc.vector.quantize_mx(
                 out=z_words[:].bitcast(FP8X4), scales=z_scales[:], in_=z_bf[:].rearrange("p v t -> p (v t)")
             )
             return z_words, z_scales
 
         def second_product(b, z_words, z_scales):
-            y = [psum.tile([P, BLOCK], F32, name="y%d_%d" % (b, t), tag=Y_BANKS[b][t]) for t in range(PACK)]
+            y = [psum.tile([P, BATCH], F32, name="y%d_%d" % (b, t), tag=Y_BANKS[b][t]) for t in range(PACK)]
             for t in range(PACK):
-                cols = slice(t * P, (t + 1) * P)
                 nc.tensor.matmul_mx(
                     out=y[t][:],
                     lhsT=w2_words[t // 2][:, (t % 2) * P : (t % 2 + 1) * P].bitcast(FP8X4),
-                    lhsT_scale=w2_scales[:, cols],
+                    lhsT_scale=w2_scales[:, t * P : (t + 1) * P],
                     rhs=z_words[:].bitcast(FP8X4),
                     rhs_scale=z_scales[:],
                     start=True,
@@ -230,80 +247,75 @@ def tile_picked_zgcnii_relu_po_kernel(
                 )
             return y
 
-        def way_out(b, y):
-            result = result_all[:, :, targets[b]]
+        def last_sums(b, y):
             for t in range(PACK):
                 nc.vector.scalar_tensor_tensor(
-                    result[:, t, :], y[t][:], turn_scaled[:, t : t + 1], u[b][:, t, :], ALU.mult, ALU.add
+                    result[:, t, targets[b]], y[t][:], turn_scaled[:, t : t + 1], u[b][:, t, :], ALU.mult, ALU.add
                 )
                 if t == 1:
-                    nc.sync.dma_start(out_0_rows[:, 0:2, targets[b]], result[:, 0:2, :])
-            if b == BLOCKS - 1:
-                nc.sync.dma_start(out_0_rows[:, 2:PACK, :], result_all[:, 2:PACK, :])
+                    nc.sync.dma_start(out_0_rows[:, 0:2, targets[b]], result[:, 0:2, targets[b]])
+            if b == BATCHES - 1:
+                nc.sync.dma_start(out_0_rows[:, 2:PACK, :], result[:, 2:PACK, :])
+            first = slice(targets[b].start, targets[b].start + OUT_SCALAR_SHARE[b])
+            nc.scalar.activation(*side_by_side(result_bf[:, first, :], result[:, :, first]), ACT.Copy, scale=1.0)
 
-            first = slice(targets[b].start, targets[b].start + SCALAR_SHARE[b])
-            nc.scalar.activation(*side_by_side(result_bf_all[:, first, :], result_all[:, :, first]), ACT.Copy, scale=1.0)
-
-        nc.scalar.activation(gate_scaled[:], gate_raw[:], ACT.Copy, scale=GATE_SCALE)
+        nc.scalar.activation(gate1_scaled[:], gate_raw[:, 1, :], ACT.Copy, scale=NEAR_OVER_CENTRE)
         nc.scalar.activation(turn_scaled[:], turn_raw[:], ACT.Copy, scale=TURN_SCALE)
         for pair in range(PACK // 2):
-            deal(nc.scalar.copy, w2_bf[:, 2 * pair : 2 * pair + 2, :, :], w2_raw, pair)
+            deal(nc.scalar.copy, w2_bf[:, 2 * pair : 2 * pair + 2, :, :], w2_raw[:], pair)
 
-        turned_sb = keep.tile([P, PACK - 1, BLOCKS, P], F32, name="turned_sb", tag="stage")
-        turned = [psum.tile([P, 2, P], F32, name="turned", tag="bank%d" % b) for b in range(BLOCKS)]
-        for half in range(2):
-            terms = look_up(half)
-            for d in range(TERMS):
-                for b in range(BLOCKS):
-                    add_turned(turned[b][:, half, :], terms, b, d)
-        for b in range(BLOCKS):
+        turned_sb = keep.tile([P, PACK - 1, BATCHES, P], F32, name="turned_sb", tag="stage")
+        turned_pair = [psum.tile([P, 2, P], F32, name="turned", tag="bank%d" % b) for b in range(BATCHES)]
+        for t in range(2):
+            add_turned([turned_pair[b][:, t, :] for b in range(BATCHES)], look_up(t))
+        for b in range(BATCHES):
             nc.scalar.copy(
                 turned_sb[:, 0:2, b, :].rearrange("v i (quarter m) -> v i quarter m", quarter=4),
-                turned[b][:].rearrange("v half (low i m) -> v i (half low) m", low=2, i=2),
+                turned_pair[b][:].rearrange("v t (part i m) -> v i (t part) m", part=2, i=2),
             )
-        for b in range(BLOCKS):
-            turn_back(b, slice(0, 2), "back%d" % b)
-        terms = look_up(PACK - 2)
-        turned_by_block = [psum.tile([P, P], F32, name="turned_block", tag="turned%d" % b) for b in range(BLOCKS)]
-        for d in range(TERMS):
-            for b in range(BLOCKS):
-                add_turned(turned_by_block[b][:], terms, b, d)
-        for b in range(BLOCKS):
+        for b in range(BATCHES):
+            turn_back(b, slice(0, 2), slice(0, 2), "back%d" % b)
+        terms = look_up(2)
+        turned_one = [psum.tile([P, P], F32, name="turned_one", tag="turned%d" % b) for b in range(BATCHES)]
+        add_turned([turned_one[b][:] for b in range(BATCHES)], terms)
+        for b in range(BATCHES):
             nc.scalar.copy(
-                turned_sb[:, PACK - 2, b, :].rearrange("v (half m) -> v half m", half=2),
-                turned_by_block[b][:].rearrange("v (half m) -> v half m", half=2)[:, ::-1, :],
+                turned_sb[:, 2, b, :].rearrange("v (half m) -> v half m", half=2),
+                turned_one[b][:].rearrange("v (half m) -> v half m", half=2)[:, ::-1, :],
             )
-        for b in range(BLOCKS):
-            turn_back(b, slice(2, 3), "bank%d" % b)
+        for b in range(BATCHES):
+            turn_back(b, slice(2, 3), slice(3, 4), "bank%d" % b)
 
-        last = h[PACK - 1]
         near = [keep.tile([P, V], F32, name="near%d" % d) for d in range(TERMS)]
-        nc.vector.tensor_tensor(near[0][:], last[:].indirect(pos1_sb[:]), gate_scaled[:, 0, :], ALU.mult)
-        list_cols = [slice(tg.start // LIST_ROWS, tg.stop // LIST_ROWS) for tg in targets]
-        for b in range(BLOCKS):
+        nc.vector.tensor_tensor(near[0][:], h[3][:].indirect(pos1_sb[:]), gate_raw[:, 0, :], ALU.mult)
+        for tg in targets:
             nc.vector.tensor_tensor(
-                near[1][:, targets[b]], last[:].indirect(pos2_sb[:, list_cols[b]]), gate_scaled[:, 1, targets[b]], ALU.mult
+                near[1][:, tg], h[3][:].indirect(pos2_sb[:, list_columns(tg)]), gate1_scaled[:, tg], ALU.mult
             )
-        for b in range(BLOCKS):
-            nc.vector.tensor_tensor(near[2][:, targets[b]], near[0][:, targets[b]], near[1][:, targets[b]], ALU.add)
-        for b in range(BLOCKS):
-            entries = cen_sb[:, list_cols[b]]
-            nc.vector.tensor_tensor(u[b][:, 2, :], last[:].indirect(entries), near[2][:, targets[b]], ALU.add)
+        for tg in targets:
+            nc.vector.scalar_tensor_tensor(
+                near[2][:, tg], near[0][:, tg], NEAR_OVER_CENTRE, near[1][:, tg], ALU.mult, ALU.add
+            )
+        for b, tg in enumerate(targets):
+            nc.vector.tensor_tensor(
+                u[b][:, 2, :], h[3][:].indirect(cen_sb[:, list_columns(tg)]), near[2][:, tg], ALU.add
+            )
 
-        z_mx = [finish_block(b) for b in range(BLOCKS)]
-        products = [second_product(b, *z_mx[b]) for b in range(BLOCKS)]
-        result_all = keep.tile([P, PACK, V], F32, name="result_all", tag="results", align_bytes=64)
-        result_bf_all = keep.tile([P, V, PACK], BF16, name="result_bf", align_bytes=64)
-        for b in range(BLOCKS):
-            way_out(b, products[b])
-        for b in range(BLOCKS):
-            rest = slice(targets[b].start + SCALAR_SHARE[b], targets[b].stop)
-            nc.vector.tensor_copy(*side_by_side(result_bf_all[:, rest, :], result_all[:, :, rest]))
-        for b in range(BLOCKS):
+        z_mx = [quantize_z(b) for b in range(BATCHES)]
+        products = [second_product(b, *z_mx[b]) for b in range(BATCHES)]
+        result = keep.tile([P, PACK, V], F32, name="result", tag="results", align_bytes=64)
+        result_bf = keep.tile([P, V, PACK], BF16, name="result_bf", align_bytes=64)
+        for b in range(BATCHES):
+            last_sums(b, products[b])
+
+        for b, tg in enumerate(targets):
+            rest = slice(tg.start + OUT_SCALAR_SHARE[b], tg.stop)
+            nc.vector.tensor_copy(*side_by_side(result_bf[:, rest, :], result[:, :, rest]))
+        for tg in targets:
             nc.vector.quantize_mx(
-                out=out_words[:, targets[b]].bitcast(FP8X4),
-                scales=out_scales[:, targets[b]],
-                in_=result_bf_all[:, targets[b], :].rearrange("p v t -> p (v t)"),
+                out=out_words[:, tg].bitcast(FP8X4),
+                scales=out_scales[:, tg],
+                in_=result_bf[:, tg, :].rearrange("p v t -> p (v t)"),
             )
         nc.sync.dma_start(out_1_words, out_words[:].bitcast(I32))
         for q in range(QUADRANTS):

@@ -18,24 +18,27 @@ ACT = mybir.ActivationFunctionType
 
 P = 128
 PACK = 4
+H_TILES = H // P
 QUADRANTS = 4
 LIST_ROWS = 16
-TERMS = 3
 BATCH = 128
 BATCHES = V // BATCH
-HALF = P // 2
 
 NEAR_SCALE = 0.54
-CENTRE_SCALE = 0.06
-NEAR_OVER_CENTRE = 9.0
+CENTRE_OVER_NEAR = 1.0 / 9.0
 Z_SCALE = 1.0 / 0.6
 TURN_SCALE = 0.4
 
+W1_PARTS = [slice(0, P), slice(P, 2 * P), slice(2 * P, H)]
+HALF = P // 2
+W2_PARTS = [slice(0, 192), slice(192, H)]
+CENTRE_TAGS = ["w1_words1", "w1_words2", "centre2", "centre3"]
 H0_PIECES = [slice(0, 256), slice(256, 384), slice(384, 512)]
-Z_SCALAR_SHARE = 80
-OUT_SCALAR_SHARE = [64, 56]
-H_TILE_COLUMN = [0, P, 3 * P, 2 * P]
-Y_BANKS = [["bank2", "bank3", "back0", "back1"], ["turned0", "turned1", "bank0", "bank1"]]
+OUT_SCALAR_SHARE = [128, 56]
+H_BANKS = ["bank3", "bank0", "bank1"]
+MIDDLE_BANKS = ["bank2", "bank0"]
+BACK_BANKS = ["early0", "early1"]
+Y_BANKS = [["bank2", "bank0", "bank3", "bank1"], ["late0", "late1", "early0", "bank2"]]
 
 
 def deal(copy, grouped, raw, pair):
@@ -45,8 +48,8 @@ def deal(copy, grouped, raw, pair):
     )
 
 
-def side_by_side(packed, row_tiles):
-    return packed.rearrange("p (c i) t -> p c t i", i=4), row_tiles.rearrange("p t (c i) -> p c t i", i=4)
+def side_by_side(packed, planes):
+    return packed.rearrange("p (c i) j -> p c j i", i=4), planes.rearrange("p j (c i) -> p c j i", i=4)
 
 
 def list_columns(entries):
@@ -68,13 +71,15 @@ def tile_picked_zgcnii_relu_po_kernel(
         x_word_table = keep.tile([P, T], U32, name="x_word_table")
         x_scale_table = keep.tile([P, T], U8, name="x_scale_table")
         w1_raw = [
-            keep.tile([P, PACK, H // 2], F32, name="w1_raw%d" % half, tag=tag, align_bytes=64)
-            for half, tag in enumerate(["w1_raw0", "term2_0"])
+            keep.tile([P, PACK, cols.stop - cols.start], F32, name="w1_raw%d" % i, align_bytes=64)
+            for i, cols in enumerate(W1_PARTS)
         ]
-        w2_raw = keep.tile([P, PACK, H], F32, name="w2_raw", tag="stage")
+        w2_raw = [
+            keep.tile([P, PACK, cols.stop - cols.start], F32, name="w2_raw%d" % i) for i, cols in enumerate(W2_PARTS)
+        ]
         turn_raw = keep.tile([P, PACK], F32, name="turn_raw")
         x_scale_rows = keep.tile([P, T], U8, name="x_scale_rows")
-        gate_raw = keep.tile([P, 2, V], F32, name="gate_raw")
+        gate_sb = keep.tile([P, 2, V], F32, name="gate_sb")
         ident = keep.tile([P, P], F32, name="ident")
 
         scale_partitions = [slice(32 * q, 32 * q + 4) for q in range(QUADRANTS)]
@@ -85,15 +90,21 @@ def tile_picked_zgcnii_relu_po_kernel(
             )
         nc.sync.dma_start(offs_sb[:], offs)
         w1_rows = w1.rearrange("(p j) c -> p j c", j=PACK)
-        nc.sync.dma_start(w1_raw[0][:], w1_rows[:, :, 0 : H // 2])
+
+        def load_w1(t):
+            nc.sync.dma_start(w1_raw[t][:], w1_rows[:, :, W1_PARTS[t]])
+
+        load_w1(0)
         nc.sync.dma_start(x_word_table[:].bitcast(I32), x_words[0].rearrange("p c r -> p (c r)").bitcast(I32))
-        nc.sync.dma_start(w1_raw[1][:], w1_rows[:, :, H // 2 : H])
+        load_w1(1)
+        load_w1(2)
         nc.sync.dma_start(cen_sb[:], cen)
-        nc.sync.dma_start(gate_raw[:], gate.rearrange("d p v -> p d v"))
         nc.sync.dma_start(pos1_sb[:], pos1)
         nc.sync.dma_start(pos2_sb[:], pos2)
-        nc.sync.dma_start(w2_raw[:], w2.rearrange("(p j) c -> p j c", j=PACK))
         nc.sync.dma_start(turn_raw[:], turn.rearrange("(p t) o -> p (t o)", t=PACK))
+        nc.sync.dma_start(gate_sb[:], gate.rearrange("d p v -> p d v"))
+        for i, cols in enumerate(W2_PARTS):
+            nc.sync.dma_start(w2_raw[i][:], w2.rearrange("(p j) c -> p j c", j=PACK)[:, :, cols])
         make_identity(nc, ident[:])
 
         nc.vector.memset(x_scale_table[:].bitcast(I32), 0)
@@ -101,223 +112,188 @@ def tile_picked_zgcnii_relu_po_kernel(
             nc.vector.tensor_copy(
                 x_scale_table[scale_partitions[q], :].bitcast(I32), x_scale_rows[scale_partitions[q], :].bitcast(I32)
             )
-        centre_share = keep.tile([P, V], F32, name="centre_share")
-        ones = keep.tile([P, V], F32, name="ones")
-        nc.vector.memset(ones[:], 1.0)
-        nc.vector.tensor_scalar_mul(centre_share[:], ones[:], 1.0 / NEAR_OVER_CENTRE)
-        z_factor = [
-            keep.tile([P, 1], F32, name="z_factor%d" % b, tag=tag, align_bytes=64)
-            for b, tag in enumerate(["w2_high", "results"])
-        ]
-        for b in range(BATCHES):
-            nc.vector.tensor_scalar_mul(z_factor[b][:], ones[:, 0:1], Z_SCALE)
-        picked_words = keep.tile([P, S], U32, name="picked_words", align_bytes=64)
         picked_scales = keep.tile([P, S], U8, name="picked_scales", align_bytes=64)
         nc.vector.tensor_copy(picked_scales[:], x_scale_table[:].indirect(offs_sb[:]))
 
-        w1_first_bf = [
-            [
-                keep.tile([P, 2, P // PACK, PACK], BF16, name="w1_bf%d_%d" % (half, part), tag=tag, align_bytes=64)
-                for part, tag in enumerate(tags)
-            ]
-            for half, tags in enumerate([["w1_bf0_0", "w1_bf0_1"], ["term0_0", "w1_bf1_1"]])
-        ]
-        w1_rest_bf = [
-            keep.tile([P, 2, HALF, PACK], BF16, name="w1_rest_bf%d" % half, align_bytes=64) for half in range(2)
-        ]
-        w1_words = keep.tile([P, H], U32, name="w1_words", tag="weights", align_bytes=64)
+        w1_bf = [keep.tile([P, P, PACK], BF16, name="w1_bf%d" % t, align_bytes=64) for t in range(H_TILES)]
+        w1_words = [keep.tile([P, P], U32, name="w1_words%d" % t, align_bytes=64) for t in range(H_TILES)]
         w1_scales = keep.tile([P, H], U8, name="w1_scales", align_bytes=64)
-        gate1_scaled = keep.tile([P, V], F32, name="gate1_scaled")
+        h = [keep.tile([P, S], F32, name="h%d" % t, align_bytes=64) for t in range(H_TILES)]
 
-        def round_first(half):
-            for part in range(2):
-                deal(nc.vector.tensor_copy, w1_first_bf[half][part][:], w1_raw[half][:, :, part * P : (part + 1) * P], 0)
+        def round_w1(t, copy):
+            if t < 2:
+                copy(*side_by_side(w1_bf[t][:], w1_raw[t][:]))
+            else:
+                deal(copy, w1_bf[t][:].rearrange("p (i m) j -> p i m j", i=2), w1_raw[2][:], t - 2)
 
-        def quantize_w1(first_column, grouped):
-            cols = slice(first_column, first_column + grouped.shape[1] * grouped.shape[2])
+        def quantize_w1(t):
             nc.vector.quantize_mx(
-                out=w1_words[:, cols].bitcast(FP8X4),
-                scales=w1_scales[:, cols],
-                in_=grouped.rearrange("p i m j -> p (i m j)"),
+                out=w1_words[t][:].bitcast(FP8X4),
+                scales=w1_scales[:, t * P : (t + 1) * P],
+                in_=w1_bf[t][:].rearrange("p m j -> p (m j)"),
             )
 
-        def quantize_first(half):
-            for part in range(2):
-                quantize_w1(H_TILE_COLUMN[half] + part * HALF, w1_first_bf[half][part][:])
+        ones = keep.tile([P, 1], F32, name="ones")
+        nc.vector.memset(ones[:], 1.0)
+        z_factor = [keep.tile([P, 1], F32, name="z_factor%d" % b, tag="u%d" % b) for b in range(BATCHES)]
+        for b in range(BATCHES):
+            nc.vector.tensor_scalar_mul(z_factor[b][:], ones[:], Z_SCALE)
 
-        h = [keep.tile([P, S], F32, name="h%d" % t) for t in range(PACK)]
-
-        def first_product(t, entries, bank, factor):
-            cols = slice(H_TILE_COLUMN[t], H_TILE_COLUMN[t] + P)
+        def first_product(t, entries, bank):
             acc = psum.tile([P, entries.stop - entries.start], F32, name="h_acc", tag=bank)
             nc.tensor.matmul_mx(
                 out=acc[:],
-                lhsT=w1_words[:, cols].bitcast(FP8X4),
-                lhsT_scale=w1_scales[:, cols],
+                lhsT=w1_words[t][:].bitcast(FP8X4),
+                lhsT_scale=w1_scales[:, t * P : (t + 1) * P],
                 rhs=picked_words[:, entries].bitcast(FP8X4),
                 rhs_scale=picked_scales[:, entries],
                 start=True,
                 stop=True,
             )
-            nc.scalar.activation(h[t][:, entries], acc[:], ACT.Relu, scale=factor)
+            return acc
 
-        round_first(0)
-        deal(nc.scalar.copy, w1_rest_bf[0][:], w1_raw[0][:], 1)
-        quantize_first(0)
-        quantize_w1(2 * P, w1_rest_bf[0][:, 0:1])
-        quantize_w1(H - HALF, w1_rest_bf[0][:, 1:2])
+        def relu(t, entries, acc):
+            nc.scalar.activation(h[t][:, entries], acc[:], ACT.Relu, scale=NEAR_SCALE)
+
+        targets = [slice(b * BATCH, (b + 1) * BATCH) for b in range(BATCHES)]
+        early = [psum.tile([P, 2, P], F32, name="early", tag="early%d" % b) for b in range(BATCHES)]
+        late = [psum.tile([P, P], F32, name="late", tag="late%d" % b) for b in range(BATCHES)]
+
+
+        def look_up(t, runs, totals):
+            centre = keep.tile([P, V], F32, name="centre%d" % t, tag=CENTRE_TAGS[t], align_bytes=64)
+            nc.scalar.activation(centre[:], h[t][:].indirect(cen_sb[:]), ACT.Copy, scale=CENTRE_OVER_NEAR)
+            terms = [[centre[:, tg]] for tg in targets]
+            for run in runs:
+                for d, pos_sb in enumerate([pos1_sb, pos2_sb]):
+                    near = keep.tile([P, run.stop - run.start], F32, name="near%d_%d_%d" % (t, d, run.start), align_bytes=64)
+                    window = h[t][:].indirect(pos_sb[:, list_columns(run)])
+                    nc.vector.tensor_tensor(near[:], window, gate_sb[:, d, run], ALU.mult)
+                    for b, tg in enumerate(targets):
+                        if run.start <= tg.start < run.stop:
+                            terms[b].append(near[:, tg.start - run.start : tg.stop - run.start])
+            for run in runs:
+                for i, d in enumerate([1, 0, 2]):
+                    for b, tg in enumerate(targets):
+                        if run.start <= tg.start < run.stop:
+                            nc.tensor.matmul(
+                                totals[b], terms[b][d], ident[:], start=(i == 0), stop=(i == 2), is_transpose=True
+                            )
+
+        round_w1(0, nc.scalar.copy)
+        quantize_w1(0)
+        picked_words = keep.tile([P, S], U32, name="picked_words", tag="w1_raw0", align_bytes=64)
         for i, piece in enumerate(H0_PIECES):
             nc.vector.tensor_copy(picked_words[:, piece], x_word_table[:].indirect(offs_sb[:, list_columns(piece)]))
-            first_product(0, piece, "bank%d" % i, NEAR_SCALE)
-        round_first(1)
-        deal(nc.scalar.copy, w1_rest_bf[1][:], w1_raw[1][:], 1)
-        quantize_first(1)
-        first_product(1, slice(0, S), "bank3", NEAR_SCALE)
-        quantize_w1(2 * P + HALF, w1_rest_bf[1][:])
-        first_product(2, slice(0, S), "bank0", NEAR_SCALE)
-        first_product(3, slice(0, S), "bank1", CENTRE_SCALE)
-
-        w2_bf = keep.tile([P, PACK, P, PACK], BF16, name="w2_bf", tag="weights", align_bytes=64)
-        w2_words = [
-            keep.tile([P, H // 2], U32, name="w2_words%d" % pair, tag=tag, align_bytes=64)
-            for pair, tag in enumerate(["w2_low", "w2_high"])
-        ]
-        w2_scales = keep.tile([P, H], U8, name="w2_scales", align_bytes=64)
+            relu(0, piece, first_product(0, piece, "bank%d" % i))
+        round_w1(1, nc.scalar.copy)
+        quantize_w1(1)
+        relu(1, slice(0, S), first_product(1, slice(0, S), H_BANKS[0]))
         turn_scaled = keep.tile([P, PACK], F32, name="turn_scaled")
+        for t in range(2, H_TILES):
+            round_w1(t, nc.vector.tensor_copy)
+        for t in range(2, H_TILES):
+            quantize_w1(t)
+        later = [first_product(t, slice(0, S), H_BANKS[t - 1]) for t in range(2, H_TILES)]
+        look_up(0, [slice(0, V)], [early[b][:, 0, :] for b in range(BATCHES)])
+        relu(2, slice(0, S), later[0])
+        look_up(1, [slice(0, V)], [early[b][:, 1, :] for b in range(BATCHES)])
+        relu(3, slice(0, S), later[1])
+        middle = [psum.tile([P, P], F32, name="middle", tag=MIDDLE_BANKS[b]) for b in range(BATCHES)]
+        look_up(2, [slice(0, V)], [middle[b][:] for b in range(BATCHES)])
+        look_up(3, targets, [late[b][:] for b in range(BATCHES)])
+
+        w2_bf = keep.tile([P, PACK, P, PACK], BF16, name="w2_bf", align_bytes=64)
+
+        def round_w2(part, copy):
+            places = slice(W2_PARTS[part].start // PACK, W2_PARTS[part].stop // PACK)
+            for pair in range(PACK // 2):
+                deal(copy, w2_bf[:, 2 * pair : 2 * pair + 2, places, :], w2_raw[part][:], pair)
+
+        round_w2(0, nc.scalar.copy)
+        all_turned = keep.tile([P, BATCHES, PACK, P], F32, name="all_turned", tag="w2_raw0")
+        turned = [all_turned[:, b] for b in range(BATCHES)]
+        back = []
+        for b in range(BATCHES):
+            nc.scalar.copy(turned[b][:, :, 0:HALF], early[b][:].rearrange("v t (q r) -> v r (t q)", r=PACK))
+            back.append(psum.tile([P, PACK, BATCH], F32, name="back", tag=BACK_BANKS[b]))
+
+        def turn_back(b, pair, sums):
+            nc.scalar.copy(turned[b][:, 2 * pair : 2 * pair + 2, HALF:P], sums.rearrange("v (i m) -> v i m", i=2))
+            for r in range(2 * pair, 2 * pair + 2):
+                nc.tensor.transpose(back[b][:, r, :], turned[b][:, r, :], ident[:])
+
+        for b in range(BATCHES):
+            turn_back(b, 0, middle[b][:])
+        for b in range(BATCHES):
+            turn_back(b, 1, late[b][:])
+
+        w2_words = keep.tile([P, H], U32, name="w2_words", align_bytes=64)
+        w2_scales = keep.tile([P, H], U8, name="w2_scales", align_bytes=64)
+        round_w2(1, nc.vector.tensor_copy)
+        for pair in range(PACK // 2):
+            cols = slice(2 * pair * P, 2 * (pair + 1) * P)
+            nc.vector.quantize_mx(
+                out=w2_words[:, cols].bitcast(FP8X4),
+                scales=w2_scales[:, cols],
+                in_=w2_bf[:, 2 * pair : 2 * pair + 2, :, :].rearrange("p t m j -> p (t m j)"),
+            )
+        nc.scalar.activation(turn_scaled[:], turn_raw[:], ACT.Copy, scale=TURN_SCALE)
+
+        z_words, z_scales, u = [], [], []
+        for b in range(BATCHES):
+            z_bf = keep.tile([P, BATCH, PACK], BF16, name="z_bf%d" % b, align_bytes=64)
+            z_words.append(keep.tile([P, BATCH], U32, name="z_words%d" % b, align_bytes=64))
+            z_scales.append(keep.tile([P, BATCH], U8, name="z_scales%d" % b, align_bytes=64))
+            nc.scalar.activation(z_bf[:], back[b][:].rearrange("p r v -> p v r"), ACT.Copy, scale=z_factor[b][:])
+            nc.vector.quantize_mx(
+                out=z_words[b][:].bitcast(FP8X4), scales=z_scales[b][:], in_=z_bf[:].rearrange("p v r -> p (v r)")
+            )
+            u.append(keep.tile([P, PACK, BATCH], F32, name="u%d" % b))
+            copy = nc.vector.tensor_copy if b == 0 else nc.scalar.copy
+            copy(u[b][:], back[b][:])
+
+
+        result = keep.tile([P, PACK, V], F32, name="result", align_bytes=64)
+        result_bf = keep.tile([P, V, PACK], BF16, name="result_bf", align_bytes=64)
         out_words = keep.tile([P, V], U32, name="out_words", align_bytes=64)
         out_scales = keep.tile([P, V], U8, name="out_scales", align_bytes=64)
-        out_0_rows = out_0.rearrange("(p t) v -> p t v", t=PACK)
-        out_1_words = out_1[0].rearrange("p c r -> p (c r)").bitcast(I32)
-        u = [keep.tile([P, PACK, BATCH], F32, name="u%d" % b) for b in range(BATCHES)]
-        targets = [slice(b * BATCH, (b + 1) * BATCH) for b in range(BATCHES)]
-
-        def look_up(t):
-            terms = [keep.tile([P, V], F32, name="term%d_%d" % (d, t), align_bytes=64) for d in range(TERMS)]
-            nc.vector.tensor_tensor(terms[0][:], h[t][:].indirect(cen_sb[:]), centre_share[:], ALU.mult)
-            nc.vector.tensor_tensor(terms[1][:], h[t][:].indirect(pos1_sb[:]), gate_raw[:, 0, :], ALU.mult)
-            nc.vector.tensor_tensor(terms[2][:], h[t][:].indirect(pos2_sb[:]), gate_raw[:, 1, :], ALU.mult)
-            return terms
-
-        def add_turned(totals, terms):
-            for d in range(TERMS):
-                for b in range(BATCHES):
-                    nc.tensor.matmul(
-                        totals[b],
-                        terms[d][:, targets[b]],
-                        ident[:],
-                        start=(d == 0),
-                        stop=(d == TERMS - 1),
-                        is_transpose=True,
-                    )
-
-        def turn_back(b, places, rows, bank):
-            back = psum.tile([P, places.stop - places.start, BATCH], F32, name="back", tag=bank)
-            for place in range(places.start, places.stop):
-                nc.tensor.transpose(back[:, place - places.start, :], turned_sb[:, place, b, :], ident[:])
-            nc.scalar.copy(u[b][:, rows, :], back[:])
-
-        def quantize_z(b):
-            z_bf = keep.tile([P, BATCH, PACK], BF16, name="z_bf%d" % b, align_bytes=64)
-            z_words = keep.tile([P, BATCH], U32, name="z_words%d" % b, align_bytes=64)
-            z_scales = keep.tile([P, BATCH], U8, name="z_scales%d" % b, align_bytes=64)
-            first, rest = slice(0, Z_SCALAR_SHARE), slice(Z_SCALAR_SHARE, BATCH)
-            nc.scalar.activation(*side_by_side(z_bf[:, first, :], u[b][:, :, first]), ACT.Copy, scale=z_factor[b][:])
-            nc.vector.tensor_scalar_mul(*side_by_side(z_bf[:, rest, :], u[b][:, :, rest]), Z_SCALE)
-            nc.vector.quantize_mx(
-                out=w2_words[b][:].bitcast(FP8X4),
-                scales=w2_scales[:, 2 * b * P : 2 * (b + 1) * P],
-                in_=w2_bf[:, 2 * b : 2 * b + 2, :, :].rearrange("p t m j -> p (t m j)"),
-            )
-            nc.vector.quantize_mx(
-                out=z_words[:].bitcast(FP8X4), scales=z_scales[:], in_=z_bf[:].rearrange("p v t -> p (v t)")
-            )
-            return z_words, z_scales
-
-        def second_product(b, z_words, z_scales):
-            y = [psum.tile([P, BATCH], F32, name="y%d_%d" % (b, t), tag=Y_BANKS[b][t]) for t in range(PACK)]
-            for t in range(PACK):
+        out_0_rows = out_0.rearrange("(p r) v -> p r v", r=PACK)
+        products = []
+        for b in range(BATCHES):
+            y = [psum.tile([P, BATCH], F32, name="y%d_%d" % (b, r), tag=Y_BANKS[b][r]) for r in range(PACK)]
+            for r in range(PACK):
                 nc.tensor.matmul_mx(
-                    out=y[t][:],
-                    lhsT=w2_words[t // 2][:, (t % 2) * P : (t % 2 + 1) * P].bitcast(FP8X4),
-                    lhsT_scale=w2_scales[:, t * P : (t + 1) * P],
-                    rhs=z_words[:].bitcast(FP8X4),
-                    rhs_scale=z_scales[:],
+                    out=y[r][:],
+                    lhsT=w2_words[:, r * P : (r + 1) * P].bitcast(FP8X4),
+                    lhsT_scale=w2_scales[:, r * P : (r + 1) * P],
+                    rhs=z_words[b][:].bitcast(FP8X4),
+                    rhs_scale=z_scales[b][:],
                     start=True,
                     stop=True,
                 )
-            return y
-
-        def last_sums(b, y):
-            for t in range(PACK):
+            products.append(y)
+        for b in range(BATCHES):
+            for r in range(PACK):
                 nc.vector.scalar_tensor_tensor(
-                    result[:, t, targets[b]], y[t][:], turn_scaled[:, t : t + 1], u[b][:, t, :], ALU.mult, ALU.add
+                    result[:, r, targets[b]], products[b][r][:], turn_scaled[:, r : r + 1], u[b][:, r, :], ALU.mult, ALU.add
                 )
-                if t == 1:
+                if r == 1:
                     nc.sync.dma_start(out_0_rows[:, 0:2, targets[b]], result[:, 0:2, targets[b]])
             if b == BATCHES - 1:
                 nc.sync.dma_start(out_0_rows[:, 2:PACK, :], result[:, 2:PACK, :])
             first = slice(targets[b].start, targets[b].start + OUT_SCALAR_SHARE[b])
             nc.scalar.activation(*side_by_side(result_bf[:, first, :], result[:, :, first]), ACT.Copy, scale=1.0)
 
-        nc.scalar.activation(gate1_scaled[:], gate_raw[:, 1, :], ACT.Copy, scale=NEAR_OVER_CENTRE)
-        nc.scalar.activation(turn_scaled[:], turn_raw[:], ACT.Copy, scale=TURN_SCALE)
-        for pair in range(PACK // 2):
-            deal(nc.scalar.copy, w2_bf[:, 2 * pair : 2 * pair + 2, :, :], w2_raw[:], pair)
-
-        turned_sb = keep.tile([P, PACK - 1, BATCHES, P], F32, name="turned_sb", tag="stage")
-        turned_pair = [psum.tile([P, 2, P], F32, name="turned", tag="bank%d" % b) for b in range(BATCHES)]
-        for t in range(2):
-            add_turned([turned_pair[b][:, t, :] for b in range(BATCHES)], look_up(t))
-        for b in range(BATCHES):
-            nc.scalar.copy(
-                turned_sb[:, 0:2, b, :].rearrange("v i (quarter m) -> v i quarter m", quarter=4),
-                turned_pair[b][:].rearrange("v t (part i m) -> v i (t part) m", part=2, i=2),
-            )
-        for b in range(BATCHES):
-            turn_back(b, slice(0, 2), slice(0, 2), "back%d" % b)
-        terms = look_up(2)
-        turned_one = [psum.tile([P, P], F32, name="turned_one", tag="turned%d" % b) for b in range(BATCHES)]
-        add_turned([turned_one[b][:] for b in range(BATCHES)], terms)
-        for b in range(BATCHES):
-            nc.scalar.copy(
-                turned_sb[:, 2, b, :].rearrange("v (half m) -> v half m", half=2),
-                turned_one[b][:].rearrange("v (half m) -> v half m", half=2)[:, ::-1, :],
-            )
-        for b in range(BATCHES):
-            turn_back(b, slice(2, 3), slice(3, 4), "bank%d" % b)
-
-        near = [keep.tile([P, V], F32, name="near%d" % d) for d in range(TERMS)]
-        nc.vector.tensor_tensor(near[0][:], h[3][:].indirect(pos1_sb[:]), gate_raw[:, 0, :], ALU.mult)
-        for tg in targets:
-            nc.vector.tensor_tensor(
-                near[1][:, tg], h[3][:].indirect(pos2_sb[:, list_columns(tg)]), gate1_scaled[:, tg], ALU.mult
-            )
-        for tg in targets:
-            nc.vector.scalar_tensor_tensor(
-                near[2][:, tg], near[0][:, tg], NEAR_OVER_CENTRE, near[1][:, tg], ALU.mult, ALU.add
-            )
-        for b, tg in enumerate(targets):
-            nc.vector.tensor_tensor(
-                u[b][:, 2, :], h[3][:].indirect(cen_sb[:, list_columns(tg)]), near[2][:, tg], ALU.add
-            )
-
-        z_mx = [quantize_z(b) for b in range(BATCHES)]
-        products = [second_product(b, *z_mx[b]) for b in range(BATCHES)]
-        result = keep.tile([P, PACK, V], F32, name="result", tag="results", align_bytes=64)
-        result_bf = keep.tile([P, V, PACK], BF16, name="result_bf", align_bytes=64)
-        for b in range(BATCHES):
-            last_sums(b, products[b])
-
-        for b, tg in enumerate(targets):
-            rest = slice(tg.start + OUT_SCALAR_SHARE[b], tg.stop)
-            nc.vector.tensor_copy(*side_by_side(result_bf[:, rest, :], result[:, :, rest]))
+        rest = slice(BATCH + OUT_SCALAR_SHARE[1], V)
+        nc.vector.tensor_copy(*side_by_side(result_bf[:, rest, :], result[:, :, rest]))
         for tg in targets:
             nc.vector.quantize_mx(
                 out=out_words[:, tg].bitcast(FP8X4),
                 scales=out_scales[:, tg],
                 in_=result_bf[:, tg, :].rearrange("p v t -> p (v t)"),
             )
-        nc.sync.dma_start(out_1_words, out_words[:].bitcast(I32))
+        nc.sync.dma_start(out_1[0].rearrange("p c r -> p (c r)").bitcast(I32), out_words[:].bitcast(I32))
         for q in range(QUADRANTS):
             queue = nc.sync if q % 2 == 0 else nc.scalar
             queue.dma_start(

@@ -101,10 +101,10 @@ def tile_picked_zgcnii_relu_po_kernel(
         nc.sync.dma_start(cen_sb[:], cen)
         nc.sync.dma_start(pos1_sb[:], pos1)
         nc.sync.dma_start(pos2_sb[:], pos2)
-        nc.sync.dma_start(turn_raw[:], turn.rearrange("(p t) o -> p (t o)", t=PACK))
         nc.sync.dma_start(gate_sb[:], gate.rearrange("d p v -> p d v"))
         for i, cols in enumerate(W2_PARTS):
             nc.sync.dma_start(w2_raw[i][:], w2.rearrange("(p j) c -> p j c", j=PACK)[:, :, cols])
+        nc.sync.dma_start(turn_raw[:], turn.rearrange("(p t) o -> p (t o)", t=PACK))
         make_identity(nc, ident[:])
 
         nc.vector.memset(x_scale_table[:].bitcast(I32), 0)
@@ -189,7 +189,6 @@ def tile_picked_zgcnii_relu_po_kernel(
         round_w1(1, nc.scalar.copy)
         quantize_w1(1)
         relu(1, slice(0, S), first_product(1, slice(0, S), H_BANKS[0]))
-        turn_scaled = keep.tile([P, PACK], F32, name="turn_scaled")
         for t in range(2, H_TILES):
             round_w1(t, nc.vector.tensor_copy)
         for t in range(2, H_TILES):
@@ -238,6 +237,7 @@ def tile_picked_zgcnii_relu_po_kernel(
                 scales=w2_scales[:, cols],
                 in_=w2_bf[:, 2 * pair : 2 * pair + 2, :, :].rearrange("p t m j -> p (t m j)"),
             )
+        turn_scaled = keep.tile([P, PACK], F32, name="turn_scaled", tag="centre3", align_bytes=64)
         nc.scalar.activation(turn_scaled[:], turn_raw[:], ACT.Copy, scale=TURN_SCALE)
 
         z_words, z_scales, u = [], [], []

@@ -133,11 +133,6 @@ def tile_picked_zgcnii_relu_po_kernel(
                 in_=w1_bf[t][:].rearrange("p m j -> p (m j)"),
             )
 
-        ones = keep.tile([P, 1], F32, name="ones")
-        nc.vector.memset(ones[:], 1.0)
-        z_factor = [keep.tile([P, 1], F32, name="z_factor%d" % b, tag="u%d" % b) for b in range(BATCHES)]
-        for b in range(BATCHES):
-            nc.vector.tensor_scalar_mul(z_factor[b][:], ones[:], Z_SCALE)
 
         def first_product(t, entries, bank):
             acc = psum.tile([P, entries.stop - entries.start], F32, name="h_acc", tag=bank)
@@ -245,7 +240,7 @@ def tile_picked_zgcnii_relu_po_kernel(
             z_bf = keep.tile([P, BATCH, PACK], BF16, name="z_bf%d" % b, align_bytes=64)
             z_words.append(keep.tile([P, BATCH], U32, name="z_words%d" % b, align_bytes=64))
             z_scales.append(keep.tile([P, BATCH], U8, name="z_scales%d" % b, align_bytes=64))
-            nc.scalar.activation(z_bf[:], back[b][:].rearrange("p r v -> p v r"), ACT.Copy, scale=z_factor[b][:])
+            nc.scalar.activation(z_bf[:], back[b][:].rearrange("p r v -> p v r"), ACT.Copy, scale=Z_SCALE)
             nc.vector.quantize_mx(
                 out=z_words[b][:].bitcast(FP8X4), scales=z_scales[b][:], in_=z_bf[:].rearrange("p v r -> p (v r)")
             )

@@ -33,6 +33,7 @@ W1_PARTS = [slice(0, P), slice(P, 2 * P), slice(2 * P, H)]
 HALF = P // 2
 W2_PARTS = [slice(0, 192), slice(192, H)]
 CENTRE_TAGS = ["w1_words1", "w1_words2", "centre2", "centre3"]
+TURNED_TAGS = ["w2_raw0", "near3_1_0"]
 H0_PIECES = [slice(0, 256), slice(256, 384), slice(384, 512)]
 OUT_SCALAR_SHARE = [128, 56]
 H_BANKS = ["bank3", "bank0", "bank1"]
@@ -75,7 +76,7 @@ def tile_picked_zgcnii_relu_po_kernel(
             for i, cols in enumerate(W1_PARTS)
         ]
         w2_raw = [
-            keep.tile([P, PACK, cols.stop - cols.start], F32, name="w2_raw%d" % i) for i, cols in enumerate(W2_PARTS)
+            keep.tile([P, PACK, cols.stop - cols.start], F32, name="w2_raw%d" % i, align_bytes=64) for i, cols in enumerate(W2_PARTS)
         ]
         turn_raw = keep.tile([P, PACK], F32, name="turn_raw")
         x_scale_rows = keep.tile([P, T], U8, name="x_scale_rows")
@@ -205,12 +206,7 @@ def tile_picked_zgcnii_relu_po_kernel(
                 deal(copy, w2_bf[:, 2 * pair : 2 * pair + 2, places, :], w2_raw[part][:], pair)
 
         round_w2(0, nc.scalar.copy)
-        all_turned = keep.tile([P, BATCHES, PACK, P], F32, name="all_turned", tag="w2_raw0")
-        turned = [all_turned[:, b] for b in range(BATCHES)]
-        back = []
-        for b in range(BATCHES):
-            nc.scalar.copy(turned[b][:, :, 0:HALF], early[b][:].rearrange("v t (q r) -> v r (t q)", r=PACK))
-            back.append(psum.tile([P, PACK, BATCH], F32, name="back", tag=BACK_BANKS[b]))
+        turned, back = [], []
 
         def turn_back(b, pair, sums):
             nc.scalar.copy(turned[b][:, 2 * pair : 2 * pair + 2, HALF:P], sums.rearrange("v (i m) -> v i m", i=2))
@@ -218,8 +214,10 @@ def tile_picked_zgcnii_relu_po_kernel(
                 nc.tensor.transpose(back[b][:, r, :], turned[b][:, r, :], ident[:])
 
         for b in range(BATCHES):
+            turned.append(keep.tile([P, PACK, P], F32, name="turned%d" % b, tag=TURNED_TAGS[b], align_bytes=64))
+            nc.scalar.copy(turned[b][:, :, 0:HALF], early[b][:].rearrange("v t (q r) -> v r (t q)", r=PACK))
+            back.append(psum.tile([P, PACK, BATCH], F32, name="back", tag=BACK_BANKS[b]))
             turn_back(b, 0, middle[b][:])
-        for b in range(BATCHES):
             turn_back(b, 1, late[b][:])
 
         w2_words = keep.tile([P, H], U32, name="w2_words", align_bytes=64)

@@ -31,7 +31,7 @@ TURN_SCALE = 0.4
 
 W1_PARTS = [slice(0, P), slice(P, 2 * P), slice(2 * P, H)]
 HALF = P // 2
-W2_PARTS = [slice(0, 192), slice(192, H)]
+W2_PARTS = [slice(0, 128), slice(128, H)]
 CENTRE_TAGS = ["w1_words1", "w1_words2", "centre2", "centre3"]
 TURNED_TAGS = ["w2_raw0", "near3_1_0"]
 H0_PIECES = [slice(0, 256), slice(256, 384), slice(384, 512)]

from contextlib import ExitStack

import concourse.mybir as mybir
from concourse.masks import make_identity

K, T, S, V, H = 512, 1024, 512, 256, 512
FLOPS = 2 * K * H * S + 2 * H * H * V

F32 = mybir.dt.float32
BF16 = mybir.dt.bfloat16
I32 = mybir.dt.int32
U32 = mybir.dt.uint32
U16 = mybir.dt.uint16
U8 = mybir.dt.uint8
FP8X4 = mybir.dt.float8_e4m3fn_x4
ALU = mybir.AluOpType
ACT = mybir.ActivationFunctionType

P = 128
PACK = 4
H_TILES = H // P
QUADRANTS = 4
LIST_ROWS = 16
BATCH = 128
BATCHES = V // BATCH

NEAR_SCALE = 0.54
CENTRE_OVER_NEAR = 1.0 / 9.0
Z_SCALE = 1.0 / 0.6
TURN_SCALE = 0.4

W1_PARTS = [slice(0, P), slice(P, 2 * P), slice(2 * P, H)]
HALF = P // 2
W2_PARTS = [slice(0, 128), slice(128, H)]
CENTRE_TAGS = ["w1_words1", "w1_words2", "centre2", "centre3"]
TURNED_TAGS = ["w2_raw0", "near3_1_0"]
H0_PIECES = [slice(0, 256), slice(256, 384), slice(384, 512)]
OUT_SCALAR_SHARE = [128, 56]
H_BANKS = ["bank3", "bank0", "bank1"]
MIDDLE_BANKS = ["bank2", "bank0"]
BACK_BANKS = ["early0", "early1"]
Y_BANKS = [["bank2", "bank0", "bank3", "bank1"], ["late0", "late1", "early0", "bank2"]]


def deal(copy, grouped, raw, pair):
    copy(
        out=grouped.rearrange("p i m j -> p m j i"),
        in_=raw.rearrange("p j (m t) -> p m j t", t=PACK)[:, :, :, 2 * pair : 2 * pair + 2],
    )


def side_by_side(packed, planes):
    return packed.rearrange("p (c i) j -> p c j i", i=4), planes.rearrange("p j (c i) -> p c j i", i=4)


def list_columns(entries):
    return slice(entries.start // LIST_ROWS, entries.stop // LIST_ROWS)


def tile_picked_zgcnii_relu_po_kernel(
    tc, x_words, x_scales, w1, w2, gate, turn, offs, cen, pos1, pos2, out_0, out_1, out_2
):
    nc = tc.nc
    with ExitStack() as ctx:
        keep = ctx.enter_context(tc.tile_pool(name="keep", bufs=1))
        psum = ctx.enter_context(tc.psum_pool(name="psum", bufs=1))

        offs_sb = keep.tile([P, S // LIST_ROWS], U16, name="offs_sb")
        cen_sb = keep.tile([P, V // LIST_ROWS], U16, name="cen_sb")
        pos1_sb = keep.tile([P, V // LIST_ROWS], U16, name="pos1_sb")
        pos2_sb = keep.tile([P, V // LIST_ROWS], U16, name="pos2_sb")
        x_word_table = keep.tile([P, T], U32, name="x_word_table")
        x_scale_table = keep.tile([P, T], U8, name="x_scale_table")
        w1_raw = [
            keep.tile([P, PACK, cols.stop - cols.start], F32, name="w1_raw%d" % i, align_bytes=64)
            for i, cols in enumerate(W1_PARTS)
        ]
        w2_raw = [
            keep.tile([P, PACK, cols.stop - cols.start], F32, name="w2_raw%d" % i, align_bytes=64) for i, cols in enumerate(W2_PARTS)
        ]
        turn_raw = keep.tile([P, PACK], F32, name="turn_raw")
        x_scale_rows = keep.tile([P, T], U8, name="x_scale_rows")
        gate_sb = keep.tile([P, 2, V], F32, name="gate_sb")
        ident = keep.tile([P, P], F32, name="ident")

        scale_partitions = [slice(32 * q, 32 * q + 4) for q in range(QUADRANTS)]
        for q in range(QUADRANTS):
            queue = nc.scalar if q < QUADRANTS // 2 else nc.sync
            queue.dma_start(
                x_scale_rows[scale_partitions[q], :].bitcast(I32), x_scales[0][4 * q : 4 * q + 4, :].bitcast(I32)
            )
        nc.sync.dma_start(offs_sb[:], offs)
        w1_rows = w1.rearrange("(p j) c -> p j c", j=PACK)

        def load_w1(t):
            nc.sync.dma_start(w1_raw[t][:], w1_rows[:, :, W1_PARTS[t]])

        load_w1(0)
        nc.sync.dma_start(x_word_table[:].bitcast(I32), x_words[0].rearrange("p c r -> p (c r)").bitcast(I32))
        load_w1(1)
        load_w1(2)
        nc.sync.dma_start(cen_sb[:], cen)
        nc.sync.dma_start(pos1_sb[:], pos1)
        nc.sync.dma_start(pos2_sb[:], pos2)
        nc.sync.dma_start(gate_sb[:], gate.rearrange("d p v -> p d v"))
        for i, cols in enumerate(W2_PARTS):
            nc.sync.dma_start(w2_raw[i][:], w2.rearrange("(p j) c -> p j c", j=PACK)[:, :, cols])
        nc.sync.dma_start(turn_raw[:], turn.rearrange("(p t) o -> p (t o)", t=PACK))
        make_identity(nc, ident[:])

        nc.vector.memset(x_scale_table[:].bitcast(I32), 0)
        for q in range(QUADRANTS):
            nc.vector.tensor_copy(
                x_scale_table[scale_partitions[q], :].bitcast(I32), x_scale_rows[scale_partitions[q], :].bitcast(I32)
            )
        picked_scales = keep.tile([P, S], U8, name="picked_scales", align_bytes=64)
        nc.vector.tensor_copy(picked_scales[:], x_scale_table[:].indirect(offs_sb[:]))

        w1_bf = [keep.tile([P, P, PACK], BF16, name="w1_bf%d" % t, align_bytes=64) for t in range(H_TILES)]
        w1_words = [keep.tile([P, P], U32, name="w1_words%d" % t, align_bytes=64) for t in range(H_TILES)]
        w1_scales = keep.tile([P, H], U8, name="w1_scales", align_bytes=64)
        h = [keep.tile([P, S], F32, name="h%d" % t, align_bytes=64) for t in range(H_TILES)]

        def round_w1(t, copy):
            if t < 2:
                copy(*side_by_side(w1_bf[t][:], w1_raw[t][:]))
            else:
                deal(copy, w1_bf[t][:].rearrange("p (i m) j -> p i m j", i=2), w1_raw[2][:], t - 2)

        def quantize_w1(t):
            nc.vector.quantize_mx(
                out=w1_words[t][:].bitcast(FP8X4),
                scales=w1_scales[:, t * P : (t + 1) * P],
                in_=w1_bf[t][:].rearrange("p m j -> p (m j)"),
            )


        def first_product(t, entries, bank):
            acc = psum.tile([P, entries.stop - entries.start], F32, name="h_acc", tag=bank)
            nc.tensor.matmul_mx(
                out=acc[:],
                lhsT=w1_words[t][:].bitcast(FP8X4),
                lhsT_scale=w1_scales[:, t * P : (t + 1) * P],
                rhs=picked_words[:, entries].bitcast(FP8X4),
                rhs_scale=picked_scales[:, entries],
                start=True,
                stop=True,
            )
            return acc

        def relu(t, entries, acc):
            nc.scalar.activation(h[t][:, entries], acc[:], ACT.Relu, scale=NEAR_SCALE)

        targets = [slice(b * BATCH, (b + 1) * BATCH) for b in range(BATCHES)]
        early = [psum.tile([P, 2, P], F32, name="early", tag="early%d" % b) for b in range(BATCHES)]
        late = [psum.tile([P, P], F32, name="late", tag="late%d" % b) for b in range(BATCHES)]


        def look_up(t, runs, totals):
            centre = keep.tile([P, V], F32, name="centre%d" % t, tag=CENTRE_TAGS[t], align_bytes=64)
            nc.scalar.activation(centre[:], h[t][:].indirect(cen_sb[:]), ACT.Copy, scale=CENTRE_OVER_NEAR)
            terms = [[centre[:, tg]] for tg in targets]
            for run in runs:
                for d, pos_sb in enumerate([pos1_sb, pos2_sb]):
                    near = keep.tile([P, run.stop - run.start], F32, name="near%d_%d_%d" % (t, d, run.start), align_bytes=64)
                    window = h[t][:].indirect(pos_sb[:, list_columns(run)])
                    nc.vector.tensor_tensor(near[:], window, gate_sb[:, d, run], ALU.mult)
                    for b, tg in enumerate(targets):
                        if run.start <= tg.start < run.stop:
                            terms[b].append(near[:, tg.start - run.start : tg.stop - run.start])
            for run in runs:
                for i, d in enumerate([1, 0, 2]):
                    for b, tg in enumerate(targets):
                        if run.start <= tg.start < run.stop:
                            nc.tensor.matmul(
                                totals[b], terms[b][d], ident[:], start=(i == 0), stop=(i == 2), is_transpose=True
                            )

        round_w1(0, nc.scalar.copy)
        quantize_w1(0)
        picked_words = keep.tile([P, S], U32, name="picked_words", tag="w1_raw0", align_bytes=64)
        for i, piece in enumerate(H0_PIECES):
            nc.vector.tensor_copy(picked_words[:, piece], x_word_table[:].indirect(offs_sb[:, list_columns(piece)]))
            relu(0, piece, first_product(0, piece, "bank%d" % i))
        round_w1(1, nc.scalar.copy)
        quantize_w1(1)
        relu(1, slice(0, S), first_product(1, slice(0, S), H_BANKS[0]))
        for t in range(2, H_TILES):
            round_w1(t, nc.vector.tensor_copy)
        for t in range(2, H_TILES):
            quantize_w1(t)
        later = [first_product(t, slice(0, S), H_BANKS[t - 1]) for t in range(2, H_TILES)]
        look_up(0, [slice(0, V)], [early[b][:, 0, :] for b in range(BATCHES)])
        relu(2, slice(0, S), later[0])
        look_up(1, [slice(0, V)], [early[b][:, 1, :] for b in range(BATCHES)])
        relu(3, slice(0, S), later[1])
        middle = [psum.tile([P, P], F32, name="middle", tag=MIDDLE_BANKS[b]) for b in range(BATCHES)]
        look_up(2, [slice(0, V)], [middle[b][:] for b in range(BATCHES)])
        look_up(3, targets, [late[b][:] for b in range(BATCHES)])

        w2_bf = keep.tile([P, PACK, P, PACK], BF16, name="w2_bf", align_bytes=64)

        def round_w2(part, copy):
            places = slice(W2_PARTS[part].start // PACK, W2_PARTS[part].stop // PACK)
            for pair in range(PACK // 2):
                deal(copy, w2_bf[:, 2 * pair : 2 * pair + 2, places, :], w2_raw[part][:], pair)

        round_w2(0, nc.scalar.copy)
        turned, back = [], []

        def turn_back(b, pair, sums):
            nc.scalar.copy(turned[b][:, 2 * pair : 2 * pair + 2, HALF:P], sums.rearrange("v (i m) -> v i m", i=2))
            for r in range(2 * pair, 2 * pair + 2):
                nc.tensor.transpose(back[b][:, r, :], turned[b][:, r, :], ident[:])

        for b in range(BATCHES):
            turned.append(keep.tile([P, PACK, P], F32, name="turned%d" % b, tag=TURNED_TAGS[b], align_bytes=64))
            nc.scalar.copy(turned[b][:, :, 0:HALF], early[b][:].rearrange("v t (q r) -> v r (t q)", r=PACK))
            back.append(psum.tile([P, PACK, BATCH], F32, name="back", tag=BACK_BANKS[b]))
            turn_back(b, 0, middle[b][:])
            turn_back(b, 1, late[b][:])

        w2_words = keep.tile([P, H], U32, name="w2_words", align_bytes=64)
        w2_scales = keep.tile([P, H], U8, name="w2_scales", align_bytes=64)
        round_w2(1, nc.vector.tensor_copy)
        for pair in range(PACK // 2):
            cols = slice(2 * pair * P, 2 * (pair + 1) * P)
            nc.vector.quantize_mx(
                out=w2_words[:, cols].bitcast(FP8X4),
                scales=w2_scales[:, cols],
                in_=w2_bf[:, 2 * pair : 2 * pair + 2, :, :].rearrange("p t m j -> p (t m j)"),
            )
        turn_scaled = keep.tile([P, PACK], F32, name="turn_scaled", tag="centre3", align_bytes=64)
        nc.scalar.activation(turn_scaled[:], turn_raw[:], ACT.Copy, scale=TURN_SCALE)

        z_words, z_scales, u = [], [], []
        for b in range(BATCHES):
            z_bf = keep.tile([P, BATCH, PACK], BF16, name="z_bf%d" % b, align_bytes=64)
            z_words.append(keep.tile([P, BATCH], U32, name="z_words%d" % b, align_bytes=64))
            z_scales.append(keep.tile([P, BATCH], U8, name="z_scales%d" % b, align_bytes=64))
            nc.scalar.activation(z_bf[:], back[b][:].rearrange("p r v -> p v r"), ACT.Copy, scale=Z_SCALE)
            nc.vector.quantize_mx(
                out=z_words[b][:].bitcast(FP8X4), scales=z_scales[b][:], in_=z_bf[:].rearrange("p v r -> p (v r)")
            )
            u.append(keep.tile([P, PACK, BATCH], F32, name="u%d" % b))
            copy = nc.vector.tensor_copy if b == 0 else nc.scalar.copy
            copy(u[b][:], back[b][:])


        result = keep.tile([P, PACK, V], F32, name="result", align_bytes=64)
        result_bf = keep.tile([P, V, PACK], BF16, name="result_bf", align_bytes=64)
        out_words = keep.tile([P, V], U32, name="out_words", align_bytes=64)
        out_scales = keep.tile([P, V], U8, name="out_scales", align_bytes=64)
        out_0_rows = out_0.rearrange("(p r) v -> p r v", r=PACK)
        products = []
        for b in range(BATCHES):
            y = [psum.tile([P, BATCH], F32, name="y%d_%d" % (b, r), tag=Y_BANKS[b][r]) for r in range(PACK)]
            for r in range(PACK):
                nc.tensor.matmul_mx(
                    out=y[r][:],
                    lhsT=w2_words[:, r * P : (r + 1) * P].bitcast(FP8X4),
                    lhsT_scale=w2_scales[:, r * P : (r + 1) * P],
                    rhs=z_words[b][:].bitcast(FP8X4),
                    rhs_scale=z_scales[b][:],
                    start=True,
                    stop=True,
                )
            products.append(y)
        for b in range(BATCHES):
            for r in range(PACK):
                nc.vector.scalar_tensor_tensor(
                    result[:, r, targets[b]], products[b][r][:], turn_scaled[:, r : r + 1], u[b][:, r, :], ALU.mult, ALU.add
                )
                if r == 1:
                    nc.sync.dma_start(out_0_rows[:, 0:2, targets[b]], result[:, 0:2, targets[b]])
            if b == BATCHES - 1:
                nc.sync.dma_start(out_0_rows[:, 2:PACK, :], result[:, 2:PACK, :])
            first = slice(targets[b].start, targets[b].start + OUT_SCALAR_SHARE[b])
            nc.scalar.activation(*side_by_side(result_bf[:, first, :], result[:, :, first]), ACT.Copy, scale=1.0)

        rest = slice(BATCH + OUT_SCALAR_SHARE[1], V)
        nc.vector.tensor_copy(*side_by_side(result_bf[:, rest, :], result[:, :, rest]))
        for tg in targets:
            nc.vector.quantize_mx(
                out=out_words[:, tg].bitcast(FP8X4),
                scales=out_scales[:, tg],
                in_=result_bf[:, tg, :].rearrange("p v t -> p (v t)"),
            )
        nc.sync.dma_start(out_1[0].rearrange("p c r -> p (c r)").bitcast(I32), out_words[:].bitcast(I32))
        for q in range(QUADRANTS):
            queue = nc.sync if q % 2 == 0 else nc.scalar
            queue.dma_start(
                out_2[0][4 * q : 4 * q + 4, :].bitcast(I32), out_scales[scale_partitions[q], :].bitcast(I32)
            )
